import numpy as np, ml_dtypes
CORES = [24,25,26,27,28,29,30,31]
N = 8
BF = ml_dtypes.bfloat16
V, Q, RO = 384, 3, 2
W = N * V
def parts(rng):
    big = rng.permutation(np.array([1.0, 1.0, 0.8, 0.8, 0.65, 0.65, 0.5, 0.5])).reshape(1, 8, 1, 1)
    am = (256 * big * rng.random((N, 8, 1, V)) * rng.random((N, 8, 16, V))).astype(np.int64)
    o = rng.permutation(8); w = np.array([12, 12, 40, 40, 80, 80, 128, 128])[o].reshape(1, 8, 1, 1); mid = np.array([10, 10, 32, 32, 57, 57, 64, 64])[o].reshape(1, 8, 1, 1)
    ph = rng.integers(-w, w + 1, (N, 8, 16, V)) & 255
    th = np.clip((mid * (0.9 + 0.2 * rng.random((N, 8, 1, 1)))).astype(np.int64) + rng.integers(-3, 4, (N, 8, 16, 1)), 0, 128)
    return am, ph, rng.integers(0, W, (N, 8, 16, V)), th
def pack(am, ph, tr, th):
    return {"amp": np.ascontiguousarray(am.reshape(N, 128, V)).astype(np.int32), "phi": np.ascontiguousarray(ph.reshape(N, 128, V)).astype(np.int32),
            "tri": np.ascontiguousarray(tr.reshape(N, 128, V)).astype(np.int32), "th": np.ascontiguousarray(th.reshape(N, 128, 1)).astype(np.int32)}
def setup_inputs(rng):
    return pack(*parts(rng))
def setup_inputs_ties(rng):
    am, ph, tr, th = parts(rng)
    am[:, :4] = rng.permutation(np.array([0, 1, 8, 255])).reshape(1, 4, 1, 1); am[:, 4:] = 64 * rng.integers(0, 2, (N, 4, 1, V))
    p = rng.permutation(np.array([0, 1, 127, 128, 129, 255, 64, 37])); size = np.abs(((p + 128) & 255) - 128)
    ph[:] = p.reshape(1, 8, 1, 1); th[:] = size.reshape(1, 8, 1, 1); th[1::2, :, int(rng.integers(0, 16)), 0] = np.maximum(size - 1, 0)
    return pack(am, ph, tr, th)
def setup_inputs_harsh(rng):
    am, ph, tr, th = parts(rng); g = rng.permutation(8); i = int(rng.integers(0, 16))
    am[:, g[1]] = 255; am[:, g[2]] = rng.integers(0, 3, (N, 16, V)); am[:, g[2], i] = rng.integers(0, 256, (N, V))
    am[int(rng.integers(0, N))] = 0; am[:, g[0]] = 0
    th[:, g[1:]] = rng.permutation(np.array([0, 0, 0, 128, 128, 5, 30])).reshape(1, 7, 1, 1)
    return pack(am, ph, tr, th)
def setup_inputs_ends(rng):
    am, ph, tr, th = parts(rng); own = np.arange(N)[:, None, None] * V + np.arange(V)[None, None, :]
    tr[:, 0] = rng.choice(np.array([0, V - 1, V, W - V, W - 1]), (N, 16, V))
    tr[:, 1, 0::2] = own
    tr[:, 2] = ((np.arange(N) + 1) % N)[:, None, None] * V + rng.integers(0, V, (N, 16, V))
    tr[:, 3, 1::2] = tr[:, 3, 0::2]
    tr[:, 4, 2::2] = tr[:, 4, 0:1]; tr[:, 4, 3::2] = tr[:, 4, 1:2]
    tr[:, 5] = own - own % Q + rng.integers(0, Q, (N, 16, V))
    return pack(am, ph, tr, th)
def setup_inputs_bright(rng):
    am, ph, tr, th = parts(rng); own = np.arange(W).reshape(N, 1, V); g = rng.permutation(8)
    sign = rng.permutation(np.array([1, -1] * 8)).reshape(1, 1, 16, 1)
    tr[:, g[:5]] = Q * rng.integers(0, W // Q, (N, 5, 16, V)) + Q - 1
    am[:, g[:5]] = rng.integers(0, 41, (1, 5, 16, 1))
    ph[:, g[:3]] = (sign * rng.integers(105, 116, (N, 3, 16, V))) & 255
    ph[:, g[3:5]] = (sign * rng.integers(62, 67, (N, 2, 16, V))) & 255
    ph[:, g[5:]] = rng.integers(-8, 9, (N, 3, 16, V)) & 255
    th[:] = 128; th[:, g[2]] = 0; th[:, g[3], :8] = 0; th[:, g[4], 8:] = 0
    for c in g[5:]:
        lose = (np.arange(Q) == rng.integers(0, Q - 1, (W // Q, 1))).reshape(W)
        live = np.flatnonzero(~lose); lose = lose.reshape(N, 1, V)
        am[:, c] = np.where(lose, rng.integers(236, 241, (N, 16, V)), rng.integers(246, 256, (N, 16, V)))
        x = live[rng.integers(0, live.size, (N, 16, V))]
        x[:, 0::2] = np.where(lose, own, x[:, 0::2])
        tr[:, c] = x
    return pack(am, ph, tr, th)
def setup_inputs_spread(rng):
    am, ph, tr, th = parts(rng)
    am = np.minimum((np.exp2(8 * rng.random((N, 8, 1, V))) * rng.random((N, 8, 16, V))).astype(np.int64), 255)
    ph = np.floor(np.exp2(7 * rng.random((N, 8, 1, V))) * (2 * rng.random((N, 8, 16, V)) - 1)).astype(np.int64) & 255
    tr = np.minimum((W * rng.random((N, 8, 16, V)) ** 3).astype(np.int64), W - 1)
    th = np.minimum(np.exp2(7 * rng.random((N, 8, 16, 1))).astype(np.int64), 128)
    return pack(am, ph, tr, th)
def check_inputs(d):
    bad = []
    for k, lo, hi in (("amp", 0, 255), ("phi", 0, 255), ("tri", 0, W - 1), ("th", 0, 128)):
        if np.min(d[k]) < lo or np.max(d[k]) > hi: bad.append("range of " + k)
    return bad
def flat(x):
    return np.ascontiguousarray(x.astype(np.int64).reshape(N, 8, 16, V).transpose(1, 2, 0, 3)).reshape(8, 16, W)
def reference(amp, phi, tri, th):
    a0, trial, tr, lim = flat(amp), flat(phi), flat(tri), flat(np.repeat(th, V, axis=2))
    rej = np.zeros((8, W), bool)
    for rnd in range(RO):
        a = np.where(rej[:, None, :], 0, a0); lev = np.full((8, W), Q - 1)
        for t in range(Q - 1):
            s = np.zeros((8, 16, W), np.int64)
            for g in range(8):
                for m in range(8): s[g] += np.minimum(a[g][:, tr[g, 2 * m]], a[g][:, tr[g, 2 * m + 1]])
            tot = np.where(rej, -1, np.add.reduce(s, axis=1))
            tot = np.where(lev == Q - 1, tot, 2 ** 24)
            first = np.argmin(tot.reshape(8, W // Q, Q), axis=2)
            gone = (np.arange(Q) == first[:, :, None]).reshape(8, W)
            lev = np.where(gone, t, lev)
            both = np.add.reduce(s, axis=0)
            a = np.where(gone[:, None, :], 0, np.minimum(np.minimum(a, s >> 3), both >> 5))
        p = np.array(trial); phased = lev == Q - 1; fail = np.zeros((8, W), bool)
        for t in range(Q - 2, -1, -1):
            at = np.stack([np.flatnonzero(lev[g] == t) for g in range(8)])
            total = np.zeros((8, 16, W // Q), np.int64); x = np.zeros((8, 16, W // Q), np.int64)
            for g in range(8):
                h = at[g]; c = trial[g][:, h]
                for m in range(8):
                    k, l = tr[g, 2 * m][h], tr[g, 2 * m + 1][h]
                    v = (phased[g][k] & phased[g][l]).astype(np.int64)
                    dl = ((p[g][:, k] + p[g][:, l] - c + 128) & 255) - 128
                    total[g] += v * dl; x[g] += v * (np.abs(dl) - lim[g][:, h])
            y = np.add.reduce(total, axis=0)
            u = (total + (y >> 3)) >> 3
            for g in range(8):
                h = at[g]; c = trial[g][:, h]; no = np.add.reduce(x[g], axis=0) > 0
                p[g][:, h] = np.where(no, c, (c + u[g]) & 255)
                phased[g][h] = ~no; fail[g][h] = no
        rej = rej | fail
    yphi = np.ascontiguousarray(p.reshape(8, 16, N, V).transpose(2, 0, 1, 3)).reshape(N, 128, V)
    ylev = np.ascontiguousarray(lev.reshape(8, N, V).transpose(1, 0, 2))
    return {"yphi": yphi.astype(np.float32), "ylev": ylev.astype(np.float32)}

@@ -1,0 +1,544 @@
+from concourse.bass import DstId, RemoteDMATransfer
+from concourse.mybir import AluOpType, ActivationFunctionType
+
+N, V, W, NB = 8, 384, 3072, 128
+H = 2.0 ** 41
+M = 49152.0
+KS = 4 * H
+CO = 2.0 ** 59
+BIG = 1e20
+
+R0_PLAN = [[[24, 40], [32, 32], [32, 32]], [[32, 32], [32, 32], [32, 32]]]
+R1_CHUNKS = [(0, 128)]
+
+SCRATCH = {}
+
+
+def _sb(names, cols, dtype):
+    for n in names.split():
+        SCRATCH[n] = ("sbuf", [128, cols], dtype)
+
+
+_sb("AI TI PI T2", V, "int32")
+_sb("THI IP IQ", 4, "int32")
+_sb("ZI YI ZJ YJ", NB, "int32")
+_sb("W0 W1 W2 W3 W4 W5 W6 W7 GA MN", W, "bfloat16")
+_sb("VV NR F2 DD", 1024, "bfloat16")
+_sb("CSU", 512, "bfloat16")
+_sb("CM", 256, "bfloat16")
+_sb("CS CSH OFF ACC", V, "bfloat16")
+_sb("mI mI8 mS32 mGp mGn mGt mMx CK CX NCS C64 VAL AS0 AS1 AC0 AC1 OL OH", NB, "bfloat16")
+_sb("TF PF RUN RST T1 GS OFC DOF LEV QF", V, "float32")
+_sb("J1 J2 J3 J4 fI fS fG pA0 pA1 pB0 pB1 B3 BD0 BD1 BD2 BE1 DL DW DH LM HH D1 D2 SG1 CU0 CU1 DT DE ONE",
+    NB, "float32")
+_sb("SC TS", 256, "float32")
+_sb("COL", 4, "float32")
+_sb("L0", V, "uint16")
+_sb("L1", 256, "uint16")
+_sb("L2 L3", NB, "uint16")
+_sb("WO", 16, "uint16")
+_sb("WA WB", 8, "uint16")
+for _i in range(8):
+    SCRATCH["P%d" % _i] = ("psum", [128, 512], "float32")
+
+SEMAPHORES = ["cV", "cA", "cP", "cG", "ldA", "ldT", "ldP", "ldH", "stP", "stL", "sent"] + ["arr%d" % i for i in range(8)]
+
+ALU = AluOpType
+ACT = ActivationFunctionType
+
+
+def rank_program(g, core, T, topo):
+    rank = T.rank_of(core)
+    if rank is None:
+        return
+    o0 = rank * V
+    queues = {"V": g.vector, "A": g.scalar, "P": g.tensor, "G": g, "S": g.sync}
+    ops = []
+    hist = {}
+    known = {q: {} for q in queues}
+    count = {q: 0 for q in queues}
+
+    def v(name, a, b, st=1):
+        return (T[name][:, a:b:st] if st != 1 else T[name][:, a:b], name, a, b, st, None)
+
+    def ind(win, off):
+        return (win[0].indirect(off[0]), win[1], win[2], win[3], 1, off)
+
+    def meet(a, b):
+        if a[0] >= b[1] or b[0] >= a[1]:
+            return False
+        return a[2] != b[2] or (a[0] - b[0]) % a[2] == 0
+
+    def add(q, fn, reads, writes, sem=None, total=16):
+        acc = []
+        for rs, wr in ((reads, False), (writes, True)):
+            for r in rs:
+                acc.append((r[1], r[2:5], wr))
+                if r[5] is not None:
+                    acc.append((r[5][1], r[5][2:5], False))
+        op = {"q": q, "fn": fn, "waits": [], "mark": False, "sem": sem, "total": total}
+        if sem is None:
+            count[q] += 1
+            op["key"], op["idx"] = q, count[q]
+        else:
+            op["key"], op["idx"] = sem, 1
+        deps = []
+        for (name, rg, wr) in acc:
+            psum = SCRATCH[name][0] == "psum"
+            for (r2, o2, w2) in hist.get(name, []):
+                clash = (wr or w2) and meet(rg, r2)
+                if psum:
+                    if o2["q"] == q and (q == "P" or not clash):
+                        continue
+                elif not clash:
+                    continue
+                deps.append(o2)
+        if q is not None:
+            kn = known[q]
+            deps.sort(key=lambda o: -o["seq"])
+            for o2 in deps:
+                if kn.get(o2["key"], 0) >= o2["idx"]:
+                    continue
+                op["waits"].append(o2)
+                o2["mark"] = True
+                for k, x in o2["clock"].items():
+                    if kn.get(k, 0) < x:
+                        kn[k] = x
+            op["clock"] = dict(kn)
+        else:
+            op["clock"] = {}
+        op["clock"][op["key"]] = op["idx"]
+        op["seq"] = len(ops)
+        ops.append(op)
+        for (name, rg, wr) in acc:
+            hist.setdefault(name, []).append((rg, op, wr))
+        return op
+
+    def rd(*xs):
+        return [x for x in xs if isinstance(x, tuple)]
+
+    def ap(x):
+        return x[0] if isinstance(x, tuple) else x
+
+    def tt(out, a, b, op):
+        add("V", lambda: g.vector.tensor_tensor(out[0], a[0], b[0], op), [a, b], [out])
+
+    def ts(out, a, s1, op0, s2=None, op1=None):
+        if op1 is None:
+            add("V", lambda: g.vector.tensor_scalar(out[0], a[0], ap(s1), None, op0), rd(a, s1), [out])
+        else:
+            add("V", lambda: g.vector.tensor_scalar(out[0], a[0], ap(s1), ap(s2), op0, op1), rd(a, s1, s2), [out])
+
+    def cp(out, a):
+        add("V", lambda: g.vector.tensor_copy(out[0], a[0]), [a], [out])
+
+    def ms(out, c):
+        add("V", lambda: g.vector.memset(out[0], c), [], [out])
+
+    def scan(out, a, b, init, op0, op1):
+        add("V", lambda: g.vector.tensor_tensor_scan(out[0], a[0], b[0], init, op0, op1), [a, b], [out])
+
+    def act(out, a, func=ACT.Copy, bias=None, scale=None):
+        kw = {}
+        if bias is not None:
+            kw["bias"] = bias
+        if scale is not None:
+            kw["scale"] = scale
+        add("A", lambda: g.scalar.activation(out[0], a[0], func, **kw), [a], [out])
+
+    def mm(out, mat, rhs, start, stop):
+        m = v(mat, 0, NB)
+        add("P", lambda: g.tensor.matmul(out[0], m[0], rhs[0], start, stop), [m, rhs], [out])
+
+    def iota(out, pattern, base, cm, flt=True):
+        if flt:
+            add("G", lambda: g.iota(out[0], pattern, base, cm, allow_small_or_imprecise_dtypes=True), [], [out])
+        else:
+            add("G", lambda: g.iota(out[0], pattern, base, cm), [], [out])
+
+    others = [T.cores[(rank + k) % N] for k in range(1, N)]
+    far = [c for c in others if topo.die(c) != topo.die(core)]
+    near = [c for c in others if topo.die(c) == topo.die(core)]
+    eng = topo.engines(core, others[0])
+    half = len(eng) // 2
+    mask_far = sum(1 << e for e in eng[0::2])
+    mask_near = sum(1 << e for e in eng[1::2])
+    sent = [0]
+
+    def send(e, a, b):
+        src = v("W%d" % e, o0 + a, o0 + b)
+
+        def fn():
+            trs = []
+            for dsts, mask in ((far, mask_far), (near, mask_near)):
+                ids = [DstId(rid=topo.addr(c)[0], pnc=topo.addr(c)[1]) for c in dsts]
+                trs.append(RemoteDMATransfer(dst_ids=ids, dma_engine_mask=mask, remote_sem=T.sem["arr%d" % e],
+                                             srcs=[src[0]], dsts=[src[0]] * len(dsts)))
+            g.remote_dma_fused(trs, local_sem=T.sem.sent)
+            return None
+        add("G", fn, [src], [])
+        sent[0] += 2 * half
+
+    def arrive(e, pieces):
+        w = [v("W%d" % e, a, b) for a, b in ((0, o0), (o0 + V, W)) if b > a]
+        add(None, None, [], w, sem="arr%d" % e, total=(N - 1) * half * pieces)
+
+    def own(e, a=0, b=V, st=1):
+        return v("W%d" % e, o0 + a, o0 + b, st)
+
+    def f(name):
+        return v(name, 0, SCRATCH[name][1][1])
+
+    add("S", lambda: g.sync.dma_start(T.AI[:], T.amp[:]), [], [f("AI")], sem="ldA")
+    add("S", lambda: g.sync.dma_start(T.TI[:], T.tri[:]), [], [f("TI")], sem="ldT")
+    add("S", lambda: g.sync.dma_start(T.PI[:], T.phi[:]), [], [f("PI")], sem="ldP")
+    iota(f("J4"), [[16, 8], [1000, 2], [2, 8]], 0, -1)
+    iota(f("J1"), [[1, 128]], 0, -1)
+    iota(v("IP", 0, 1), [[0, 1]], 0, 1, False)
+    iota(f("J2"), [[0, 8], [1, 16]], 0, 0)
+    iota(f("J3"), [[1, 8], [0, 16]], 0, 0)
+    ms(f("CSU"), -31.0 / 64)
+    ms(f("CM"), M)
+    ms(f("CK"), H)
+    ms(f("CX"), -KS / 2)
+    for n_, c_ in (("pA0", 0.0), ("pA1", 1000.0), ("pB0", -1.0), ("pB1", 999.0)):
+        ts(f(n_), f("J4"), c_, ALU.is_equal)
+    ts(f("fI"), f("J1"), 0.0, ALU.is_equal)
+    cp(own(0), f("AI"))
+    send(0, 0, V)
+    arrive(0, 1)
+    iota(f("QF"), [[0, 128], [1, 3]], 0, 0)
+    iota(f("B3"), [[3, 128]], 0, 0)
+    add("G", lambda: g.dma_start(T.THI[:, 0:1], T.th[:], allow_slow_non_contiguous=True), [], [v("THI", 0, 1)], sem="ldH")
+
+    def permute(src, n, dst):
+        h = n // 2
+        for k, x in enumerate("AB"):
+            mm(v("P7", k * h, k * h + h), "p%s0" % x, v(src, 0, n, 2), True, False)
+            mm(v("P7", k * h, k * h + h), "p%s1" % x, v(src, 1, n, 2), False, True)
+        if dst:
+            cp(v(dst, 0, n), v("P7", 0, n))
+
+    def r0_init():
+        h0 = 0
+        for k, ch in enumerate(R0_PLAN):
+            n = sum(sum(x) for x in ch)
+            mm(v("P%d" % k, 0, 2 * n), "mI", v("CSU", 0, 2 * n), True, False)
+            mm(v("P%d" % (2 + k), 0, n), "mI", v("OFF", h0, h0 + n), True, False)
+            h0 += n
+
+    cp(f("TF"), f("TI"))
+    permute("TF", V, None)
+    ts(v("IQ", 0, 1), v("IP", 0, 1), 15, ALU.bitwise_and)
+    ts(v("IQ", 1, 2), v("IP", 0, 1), 4, ALU.arith_shift_right)
+    ms(f("RST"), -BIG)
+    cp(v("COL", 0, 2), v("IQ", 0, 2))
+    ms(v("RST", 0, V, 3), BIG)
+    act(f("mI"), f("fI"))
+    act(f("mI8"), f("fI"), ACT.Identity, scale=0.125)
+    act(f("J1"), f("fI"), ACT.Identity, scale=8.0)
+    ts(f("fS"), f("J2"), v("COL", 0, 1), ALU.is_equal)
+    ts(f("fG"), f("J3"), v("COL", 1, 2), ALU.is_equal, KS, ALU.mult)
+    cp(f("L0"), v("P7", 0, V))
+    act(f("mS32"), f("fS"), ACT.Identity, scale=1.0 / 32)
+    act(f("mGp"), f("fG"))
+    act(f("OFF"), f("QF"), ACT.Identity, scale=H)
+    r0_init()
+    act(f("mGn"), f("fG"), ACT.Identity, scale=-1.0)
+    act(f("J2"), f("fS"), ACT.Identity, bias=-1.0)
+    act(f("OFC"), f("QF"), ACT.Identity, bias=-3 * CO, scale=CO)
+    act(f("DOF"), f("QF"), ACT.Identity, bias=3 * CO, scale=H - CO)
+    cp(f("PF"), f("PI"))
+    tt(f("mMx"), f("J1"), f("fS"), ALU.add)
+    ts(v("P6", 0, V), f("PF"), 128.0, ALU.is_gt, -256.0, ALU.mult)
+    tt(f("BD0"), f("B3"), f("fS"), ALU.mult)
+    tt(f("CS"), v("P6", 0, V), f("PF"), ALU.add)
+    tt(f("BE1"), f("BD0"), f("fS"), ALU.add)
+    ms(f("ONE"), 1.0)
+    tt(f("BD1"), f("BE1"), f("J2"), ALU.add)
+    ms(f("ACC"), 1.0)
+    tt(f("BD2"), f("BD1"), f("fS"), ALU.add)
+
+    first = [True]
+
+    def pair(win, lst, la, lb, cols, pos, op):
+        n = 16 * cols
+        ga = v("GA", pos, pos + n)
+        w = v(win, 0, W)
+        if first[0]:
+            cp(ga, ind(w, v(lst, la, la + cols)))
+            first[0] = False
+        else:
+            act(ga, ind(w, v(lst, la, la + cols)))
+        tt(v("MN", pos, pos + n), ind(w, v(lst, lb, lb + cols)), ga, op)
+
+    def round0(e):
+        win = "W%d" % e
+        first[0] = True
+        pending = [None]
+
+        def post(k, h0, n):
+            su, kk = "P%d" % k, "P%d" % (2 + k)
+            scan(v("RUN", h0, h0 + n), v("RST", h0, h0 + n), v(kk, 0, n), 0.0, ALU.max, ALU.min)
+            for q in range(3):
+                tt(v("P4", h0 + q, h0 + n, 3), v(kk, q, n, 3), v("RUN", h0 + 2, h0 + n, 3), ALU.subtract)
+            tt(v("T1", h0, h0 + n), v(su, 0, n), own(e, h0, h0 + n), ALU.min)
+            tt(v("T2", h0, h0 + n), v(su, n, 2 * n), v("T1", h0, h0 + n), ALU.min)
+            tt(own(e + 1, h0, h0 + n), v("P4", h0, h0 + n), v("T2", h0, h0 + n), ALU.min)
+            send(e + 1, h0, h0 + n)
+
+        h = 0
+        for k, ch in enumerate(R0_PLAN):
+            h0, n = h, sum(sum(x) for x in ch)
+            for gi, grp in enumerate(ch):
+                a = h
+                for w in grp:
+                    pair(win, "L0", h // 2, V // 2 + h // 2, w // 2, 8 * h, ALU.min)
+                    h += w
+                    if pending[0] is not None:
+                        post(*pending[0])
+                        pending[0] = None
+                last = gi == len(ch) - 1
+                for m in range(8):
+                    mm(v("P%d" % (2 + k), a - h0, h - h0), "mGp", v("MN", 8 * a + m, 8 * h, 8), False, last and m == 7)
+                for m in range(8):
+                    mm(v("P%d" % k, a - h0, h - h0), "mI8", v("MN", 8 * a + m, 8 * h, 8), False, False)
+                for m in range(8):
+                    mm(v("P%d" % k, n + a - h0, n + h - h0), "mS32", v("MN", 8 * a + m, 8 * h, 8), False, last and m == 7)
+            pending[0] = (k, h0, n)
+        post(*pending[0])
+        arrive(e + 1, len(R0_PLAN))
+
+    def prep_round1(ps):
+        tt(f("DL"), f("BD1"), v("P4", 0, V, 3), ALU.subtract)
+        tt(f("DW"), v("RUN", 1, V, 3), v("RUN", 2, V, 3), ALU.subtract)
+        act(f("GS"), v("P4", 0, V))
+        scan(v("SC", 0, NB), f("BD0"), f("DL"), 0.0, ALU.max, ALU.max)
+        tt(f("DH"), f("BD2"), f("DW"), ALU.subtract)
+        scan(v("SC", NB, 2 * NB), f("BE1"), f("DH"), 0.0, ALU.max, ALU.max)
+        cp(f("WO"), v("SC", 15, 256, 16))
+        cp(f("TS"), ind(f("TF"), f("WO")))
+        act(v("P4", 0, V), f("GS"), ACT.Identity, bias=H, scale=-2.0)
+        act(f("SG1"), v("GS", 0, V, 3), ACT.Sign, bias=1.0, scale=-1.0)
+        if ps:
+            act(f("OL"), ind(f("OFF"), v("WO", 0, 8)), ACT.Identity, scale=-1.0)
+            act(f("OH"), ind(f("OFF"), v("WO", 8, 16)))
+        permute("TS", 256, None)
+        tt(f("CSH"), v("P4", 0, V), f("CS"), ALU.max)
+        tt(f("LM"), f("BD0"), f("DL"), ALU.max)
+        tt(f("HH"), f("BE1"), f("DH"), ALU.max)
+        cp(f("L1"), v("P7", 0, 256))
+        for k, (b0, b1) in enumerate(R1_CHUNKS):
+            d = v("P%d" % (5 + k), b0, b1)
+            if ps:
+                mm(d, "mI", v("OL", b0, b1), True, False)
+                mm(d, "mI", v("OH", b0, b1), False, False)
+            else:
+                mm(d, "mI", v("CK", b0, b1), True, False)
+
+    def round1(e):
+        win = "W%d" % e
+        first[0] = True
+        pending = [None]
+
+        def post(k, b0, b1):
+            p = "P%d" % (5 + k)
+            E, F, Y = v(p, 128 + b0, 128 + b1), v(p, 256 + b0, 256 + b1), v(p, 384 + b0, 384 + b1)
+            ts(E, v(p, b0, b1), H, ALU.min, -H, ALU.max)
+            ts(F, v(p, b0, b1), -1.0, ALU.mult, H, ALU.min)
+            tt(Y, E, v("SG1", b0, b1), ALU.mult)
+            for q, x in ((0, E), (2, F), (1, Y)):
+                tt(own(e + 1, 3 * b0 + q, 3 * b1, 3), x, v("CSH", 3 * b0 + q, 3 * b1, 3), ALU.max)
+            send(e + 1, 3 * b0, 3 * b1)
+
+        for k, (b0, b1) in enumerate(R1_CHUNKS):
+            for side in (0, 1):
+                for a in range(b0, b1, 64):
+                    sizes = (24, 40) if first[0] else (32, 32)
+                    b = a
+                    for w in sizes:
+                        c = 64 * side + b // 2
+                        pair(win, "L1", c, 128 + c, w // 2, 16 * c, ALU.min)
+                        b += w
+                        if pending[0] is not None:
+                            post(*pending[0])
+                            pending[0] = None
+                    last = side == 1 and a + 64 == b1
+                    base = 1024 * side
+                    for m in range(8):
+                        mm(v("P%d" % (5 + k), a, a + 64), "mGp" if side else "mGn",
+                           v("MN", base + 8 * a + m, base + 8 * a + 512, 8), False, last and m == 7)
+            pending[0] = (k, b0, b1)
+        post(*pending[0])
+        arrive(e + 1, len(R1_CHUNKS))
+
+    def prep_level(wo, lst, need_z):
+        cp(f(wo), v("SC", 15, NB, 16))
+        cp(v("TS", 0, NB), ind(f("TF"), f(wo)))
+        act(f("NCS"), ind(f("CS"), f(wo)), ACT.Identity, scale=-1.0)
+        if need_z:
+            act(f("C64"), f("NCS"), ACT.Identity, scale=-64.0)
+        permute("TS", NB, lst)
+        for k in range(4):
+            mm(v("P%d" % k, 0, 256), "mI", f("CM"), True, False)
+            for m in range(8):
+                mm(v("P%d" % k, m, 256, 8), "mI", v("NCS", 32 * k, 32 * k + 32), False, False)
+        if need_z:
+            mm(v("P5", 0, NB), "mI", f("C64"), True, False)
+        mm(v("P6", 0, NB), "mI", f("CX"), True, False)
+
+    def level(e, lst, need_z):
+        w = v("W%d" % e, 0, W)
+
+        def q(name, k):
+            return v(name, 256 * k, 256 * k + 256)
+
+        def e_(k):
+            return v("P%d" % k, 0, 256)
+
+        def ga(a, b, fn=act):
+            fn(v("GA", 16 * a, 16 * b), ind(w, v(lst, a, b)))
+
+        def s(a, b):
+            tt(v("MN", 16 * a, 16 * b), ind(w, v(lst, 64 + a, 64 + b)), v("GA", 16 * a, 16 * b), ALU.add)
+            if b % 16 == 0:
+                mm(e_(b // 16 - 1), "mI", q("MN", b // 16 - 1), False, True)
+
+        def r(k):
+            act(q("NR", k), e_(k), ACT.Identity, bias=-0.5, scale=-1.0)
+
+        def d(k):
+            tt(q("DD", k), e_(k), q("NR", k), ALU.add)
+
+        def ab(k):
+            act(q("F2", k), q("DD", k), ACT.Abs)
+
+        def vv(h):
+            ts(v("VV", 512 * h, 512 * h + 512), v("MN", 512 * h, 512 * h + 512), 1000.0, ALU.is_lt)
+            summ("P6", "mGt", "VV", h)
+
+        def summ(bank, mat, src, h, stop=False):
+            for m in range(8):
+                mm(v(bank, 64 * h, 64 * h + 64), mat, v(src, 512 * h + m, 512 * h + 512, 8), False, stop and m == 7)
+
+        ga(0, 8, cp)
+        ga(8, 16)
+        ga(16, 32)
+        ga(32, 48)
+        s(0, 8)
+        s(8, 16)
+        s(16, 32)
+        r(0)
+        ga(48, 64)
+        s(32, 48)
+        d(0)
+        r(1)
+        s(48, 64)
+        r(2)
+        ab(0)
+        d(1)
+        r(3)
+        if need_z:
+            summ("P5", "mMx", "DD", 0)
+        vv(0)
+        d(2)
+        ab(1)
+        summ("P6", "mGp", "F2", 0)
+        d(3)
+        ab(2)
+        if need_z:
+            summ("P5", "mMx", "DD", 1, True)
+        vv(1)
+        ab(3)
+        summ("P6", "mGp", "F2", 1, True)
+
+    Z, X = v("P5", 0, NB), v("P6", 0, NB)
+
+    def new_phase(zi, yi, shift):
+        ts(f(zi), Z, 64.0 * shift, ALU.add)
+        ts(f(yi), f(zi), 6, ALU.arith_shift_right, 255, ALU.bitwise_and)
+
+    for ps in range(2):
+        e = 4 * ps
+        round0(e)
+        prep_round1(ps)
+        round1(e + 1)
+        for k, (b0, b1) in enumerate(R1_CHUNKS):
+            tt(v("D1", b0, b1), v("P%d" % (5 + k), 256 + b0, 256 + b1), v("HH", b0, b1), ALU.min)
+        scan(v("SC", 0, NB), f("LM"), f("D1"), 0.0, ALU.max, ALU.max)
+        prep_level("WA", "L2", True)
+        act(own(e + 3), own(e + 2))
+        if ps == 0:
+            cp(v("COL", 2, 3), v("THI", 0, 1))
+            act(f("AS1"), ind(own(0), f("WA")))
+            act(own(4), own(0))
+            ts(f("mGt"), f("fG"), v("COL", 2, 3), ALU.mult, -1.0, ALU.mult)
+        else:
+            act(f("CU1"), ind(f("PF"), f("WA")))
+        tt(f("D1"), f("BD1"), v("GS", 1, V, 3), ALU.subtract)
+        tt(f("D2"), f("BD2"), v("GS", 2, V, 3), ALU.subtract)
+        tt(f("D1"), f("D1"), f("D2"), ALU.max)
+        scan(v("SC", 0, NB), f("BD0"), f("D1"), 0.0, ALU.max, ALU.max)
+        level(e + 2, "L2", True)
+        new_phase("ZI", "YI", 127)
+        ts(v("P6", NB, 2 * NB), X, H, ALU.min, -127.0, ALU.max)
+        tt(f("VAL"), v("P6", NB, 2 * NB), f("YI"), ALU.add)
+        cp(ind(own(e + 3), f("WA")), f("VAL"))
+        send(e + 3, 0, V)
+        arrive(e + 3, 1)
+        ts(f("AC1"), X, 0.0, ALU.is_le)
+        if ps:
+            cp(f("ZJ"), Z)
+        prep_level("WB", "L3", ps == 1)
+        if ps == 0:
+            act(f("AS0"), ind(own(0), f("WB")))
+            tt(ind(own(4), f("WA")), f("AS1"), f("AC1"), ALU.mult)
+            cp(ind(f("ACC"), f("WA")), f("AC1"))
+            level(e + 3, "L3", False)
+            ts(f("AC0"), X, 0.0, ALU.is_le)
+            tt(ind(own(4), f("WB")), f("AS0"), f("AC0"), ALU.mult)
+            send(4, 0, V)
+            arrive(4, 1)
+            cp(ind(f("ACC"), f("WB")), f("AC0"))
+            tt(f("T1"), f("ACC"), f("DOF"), ALU.mult)
+            tt(f("OFF"), f("T1"), f("OFC"), ALU.add)
+            r0_init()
+        else:
+            act(f("CU0"), ind(f("PF"), f("WB")))
+            act(v("P4", 0, NB), f("CU0"))
+            ts(f("LEV"), f("GS"), 2.0, ALU.min)
+            ts(f("YJ"), f("ZJ"), 6, ALU.arith_shift_right, 255, ALU.bitwise_and)
+            cp(ind(f("LEV"), f("WA")), f("ONE"))
+            tt(f("DT"), f("YJ"), f("CU1"), ALU.subtract)
+            add("S", lambda: g.sync.dma_start(T.ylev[:], T.LEV[0:128:16, :]), [f("LEV")], [], sem="stL")
+            tt(f("DE"), f("DT"), f("AC1"), ALU.mult)
+            tt(ind(f("PF"), f("WA")), f("DE"), f("CU1"), ALU.add)
+            level(e + 3, "L3", True)
+            new_phase("ZI", "YI", 0)
+            tt(f("DT"), f("YI"), v("P4", 0, NB), ALU.subtract)
+            ts(v("P6", NB, 2 * NB), X, 0.0, ALU.is_le)
+            tt(f("DE"), v("P6", NB, 2 * NB), f("DT"), ALU.mult)
+            tt(ind(f("PF"), f("WB")), f("DE"), f("CU0"), ALU.add)
+            add("S", lambda: g.sync.dma_start(T.yphi[:], T.PF[:]), [f("PF")], [], sem="stP")
+
+    n = {q: 0 for q in queues}
+    for op in ops:
+        if op["sem"] is None:
+            if op["mark"]:
+                n[op["q"]] += 1
+            op["wait"] = ("c" + op["q"], n[op["q"]])
+        else:
+            op["wait"] = (op["sem"], op["total"])
+    for op in ops:
+        if op["q"] is None:
+            continue
+        for o2 in op["waits"]:
+            queues[op["q"]].wait_ge(T.sem[o2["wait"][0]], o2["wait"][1])
+        ins = op["fn"]()
+        if op["sem"] is not None:
+            ins.then_inc(T.sem[op["sem"]], 16)
+        elif op["mark"]:
+            ins.then_inc(T.sem["c" + op["q"]], 1)
+    g.wait_ge(T.sem.sent, sent[0])
+    g.sync.wait_ge(T.sem.stL, 16)
+    g.sync.wait_ge(T.sem.stP, 16)

@@ -8,8 +8,11 @@ KS = 4 * H
 CO = 2.0 ** 59
 BIG = 1e20
 
-R0_PLAN = [[[24, 40], [32, 32], [32, 32]], [[32, 32], [32, 32], [32, 32]]]
-R1_CHUNKS = [(0, 128)]
+R0_PLAN = [[[24, 40], [32, 32], [32, 24], [32, 24]], [[72]], [[40, 32]]]
+SU, UU, KK = ("P0", "P1", "P5"), ("P0", "P1", "P7"), ("P2", "P3", "P6")
+R1_CHUNKS = [(0, 80), (80, 128)]
+R1_PIECES = [[(24, 28, 28), (40, 40)], [(48,), (48,)]]
+ORDER = "g0 g1 g2 g3 s0 s1 s2 r0 g4 s3 d0 r1 s4 r2 a0 d1 r3 z0 v0 d2 a1 x0 d3 a2 z1 v1 a3 x1"
 
 SCRATCH = {}
 
@@ -26,22 +29,26 @@ _sb("W0 W1 W2 W3 W4 W5 W6 W7 GA MN", W, "bfloat16")
 _sb("VV NR F2 DD", 1024, "bfloat16")
 _sb("CSU", 512, "bfloat16")
 _sb("CM", 256, "bfloat16")
-_sb("CS CSH OFF ACC", V, "bfloat16")
-_sb("mI mI8 mS32 mGp mGn mGt mMx CK CX NCS C64 VAL AS0 AS1 AC0 AC1 OL OH", NB, "bfloat16")
-_sb("TF PF RUN RST T1 GS OFC DOF LEV QF", V, "float32")
-_sb("J1 J2 J3 J4 fI fS fG pA0 pA1 pB0 pB1 B3 BD0 BD1 BD2 BE1 DL DW DH LM HH D1 D2 SG1 CU0 CU1 DT DE ONE",
+_sb("CS CSH OFF OFC COX", V, "bfloat16")
+_sb("mI mI8 mS32 mGp mGn mGt mMx CK CX NCS C64 VAL AS0 AS1 AC0 AC1 OL OH OC0 OC1 RJ0 RJ1", NB, "bfloat16")
+_sb("TF PF RUN RST T1 GS LEV QF", V, "float32")
+_sb("J1 J2 J3 J4 fI fS fG pA0 pA1 pB0 pB1 B3 BD0 BD1 BD2 BE1 DL DH LM HH D1 SG1 CU0 CU1 DT DE ONE TB",
     NB, "float32")
 _sb("SC TS", 256, "float32")
 _sb("COL", 4, "float32")
+_sb("SM", 16, "float32")
+_sb("CB", 8, "float32")
 _sb("L0", V, "uint16")
 _sb("L1", 256, "uint16")
 _sb("L2 L3", NB, "uint16")
 _sb("WO", 16, "uint16")
 _sb("WA WB", 8, "uint16")
+_sb("WB1", 4, "uint16")
 for _i in range(8):
     SCRATCH["P%d" % _i] = ("psum", [128, 512], "float32")
 
-SEMAPHORES = ["cV", "cA", "cP", "cG", "ldA", "ldT", "ldP", "ldH", "stP", "stL", "sent"] + ["arr%d" % i for i in range(8)]
+SEMAPHORES = (["cV", "cA", "cP", "cG", "ldA", "ldT", "ldP", "ldH", "stP0", "stP1", "stL", "sent"]
+              + ["arr%d" % i for i in range(8)])
 
 ALU = AluOpType
 ACT = ActivationFunctionType
@@ -175,7 +182,6 @@ def rank_program(g, core, T, topo):
                 trs.append(RemoteDMATransfer(dst_ids=ids, dma_engine_mask=mask, remote_sem=T.sem["arr%d" % e],
                                              srcs=[src[0]], dsts=[src[0]] * len(dsts)))
             g.remote_dma_fused(trs, local_sem=T.sem.sent)
-            return None
         add("G", fn, [src], [])
         sent[0] += 2 * half
 
@@ -195,68 +201,73 @@ def rank_program(g, core, T, topo):
     iota(f("J4"), [[16, 8], [1000, 2], [2, 8]], 0, -1)
     iota(f("J1"), [[1, 128]], 0, -1)
     iota(v("IP", 0, 1), [[0, 1]], 0, 1, False)
-    iota(f("J2"), [[0, 8], [1, 16]], 0, 0)
-    iota(f("J3"), [[1, 8], [0, 16]], 0, 0)
     ms(f("CSU"), -31.0 / 64)
     ms(f("CM"), M)
-    ms(f("CK"), H)
-    ms(f("CX"), -KS / 2)
     for n_, c_ in (("pA0", 0.0), ("pA1", 1000.0), ("pB0", -1.0), ("pB1", 999.0)):
         ts(f(n_), f("J4"), c_, ALU.is_equal)
-    ts(f("fI"), f("J1"), 0.0, ALU.is_equal)
     cp(own(0), f("AI"))
     send(0, 0, V)
     arrive(0, 1)
+    iota(f("J2"), [[0, 8], [1, 16]], 0, 0)
+    iota(f("J3"), [[1, 8], [0, 16]], 0, 0)
     iota(f("QF"), [[0, 128], [1, 3]], 0, 0)
     iota(f("B3"), [[3, 128]], 0, 0)
+    iota(v("SM", 0, 8), [[16, 8]], 0, 0)
     add("G", lambda: g.dma_start(T.THI[:, 0:1], T.th[:], allow_slow_non_contiguous=True), [], [v("THI", 0, 1)], sem="ldH")
 
-    def permute(src, n, dst):
+    def permute(src, n):
         h = n // 2
         for k, x in enumerate("AB"):
             mm(v("P7", k * h, k * h + h), "p%s0" % x, v(src, 0, n, 2), True, False)
             mm(v("P7", k * h, k * h + h), "p%s1" % x, v(src, 1, n, 2), False, True)
-        if dst:
-            cp(v(dst, 0, n), v("P7", 0, n))
 
-    def r0_init():
+    def r0_init(ps):
         h0 = 0
         for k, ch in enumerate(R0_PLAN):
             n = sum(sum(x) for x in ch)
-            mm(v("P%d" % k, 0, 2 * n), "mI", v("CSU", 0, 2 * n), True, False)
-            mm(v("P%d" % (2 + k), 0, n), "mI", v("OFF", h0, h0 + n), True, False)
+            mm(v(SU[k], 0, 2 * n), "mI", v("CSU", 0, 2 * n), True, False)
+            if UU[k] != SU[k]:
+                mm(v(UU[k], 0, 2 * n), "mI", v("CSU", 0, 2 * n), True, False)
+            mm(v(KK[k], 0, n), "mI", v("OFF", h0, h0 + n), True, False)
+            h0 += n
+        h0 = 0
+        for k, ch in enumerate(R0_PLAN if ps else []):
+            n = sum(sum(x) for x in ch)
+            mm(v(KK[k], 0, n), "mI", v("COX", h0, h0 + n), False, False)
             h0 += n
 
+    ts(f("fI"), f("J1"), 0.0, ALU.is_equal)
     cp(f("TF"), f("TI"))
-    permute("TF", V, None)
+    permute("TF", V)
     ts(v("IQ", 0, 1), v("IP", 0, 1), 15, ALU.bitwise_and)
     ts(v("IQ", 1, 2), v("IP", 0, 1), 4, ALU.arith_shift_right)
-    ms(f("RST"), -BIG)
+    cp(f("PF"), f("PI"))
     cp(v("COL", 0, 2), v("IQ", 0, 2))
-    ms(v("RST", 0, V, 3), BIG)
     act(f("mI"), f("fI"))
     act(f("mI8"), f("fI"), ACT.Identity, scale=0.125)
     act(f("J1"), f("fI"), ACT.Identity, scale=8.0)
+    act(f("ONE"), f("fI"), ACT.Identity, bias=1.0, scale=0.0)
+    act(f("CK"), f("fI"), ACT.Identity, bias=H, scale=0.0)
+    act(f("CX"), f("fI"), ACT.Identity, bias=-KS / 2, scale=0.0)
+    ts(v("P4", 0, V), f("PF"), 128.0, ALU.is_gt, -256.0, ALU.mult)
     ts(f("fS"), f("J2"), v("COL", 0, 1), ALU.is_equal)
     ts(f("fG"), f("J3"), v("COL", 1, 2), ALU.is_equal, KS, ALU.mult)
+    tt(f("CS"), v("P4", 0, V), f("PF"), ALU.add)
     cp(f("L0"), v("P7", 0, V))
     act(f("mS32"), f("fS"), ACT.Identity, scale=1.0 / 32)
     act(f("mGp"), f("fG"))
-    act(f("OFF"), f("QF"), ACT.Identity, scale=H)
-    r0_init()
-    act(f("mGn"), f("fG"), ACT.Identity, scale=-1.0)
     act(f("J2"), f("fS"), ACT.Identity, bias=-1.0)
+    act(f("OFF"), f("QF"), ACT.Identity, scale=H)
+    r0_init(0)
+    act(f("RST"), f("QF"), ACT.Identity, bias=BIG, scale=-2 * BIG)
+    act(f("mGn"), f("fG"), ACT.Identity, scale=-1.0)
     act(f("OFC"), f("QF"), ACT.Identity, bias=-3 * CO, scale=CO)
-    act(f("DOF"), f("QF"), ACT.Identity, bias=3 * CO, scale=H - CO)
-    cp(f("PF"), f("PI"))
+    act(f("COX"), f("QF"), ACT.Identity, scale=0.0)
     tt(f("mMx"), f("J1"), f("fS"), ALU.add)
-    ts(v("P6", 0, V), f("PF"), 128.0, ALU.is_gt, -256.0, ALU.mult)
     tt(f("BD0"), f("B3"), f("fS"), ALU.mult)
-    tt(f("CS"), v("P6", 0, V), f("PF"), ALU.add)
+    ts(f("CB"), v("SM", 0, 8), v("COL", 0, 1), ALU.add, 9.0, ALU.mult)
     tt(f("BE1"), f("BD0"), f("fS"), ALU.add)
-    ms(f("ONE"), 1.0)
     tt(f("BD1"), f("BE1"), f("J2"), ALU.add)
-    ms(f("ACC"), 1.0)
     tt(f("BD2"), f("BD1"), f("fS"), ALU.add)
 
     first = [True]
@@ -275,18 +286,22 @@ def rank_program(g, core, T, topo):
     def round0(e):
         win = "W%d" % e
         first[0] = True
-        pending = [None]
 
-        def post(k, h0, n):
-            su, kk = "P%d" % k, "P%d" % (2 + k)
-            scan(v("RUN", h0, h0 + n), v("RST", h0, h0 + n), v(kk, 0, n), 0.0, ALU.max, ALU.min)
-            for q in range(3):
-                tt(v("P4", h0 + q, h0 + n, 3), v(kk, q, n, 3), v("RUN", h0 + 2, h0 + n, 3), ALU.subtract)
-            tt(v("T1", h0, h0 + n), v(su, 0, n), own(e, h0, h0 + n), ALU.min)
-            tt(v("T2", h0, h0 + n), v(su, n, 2 * n), v("T1", h0, h0 + n), ALU.min)
-            tt(own(e + 1, h0, h0 + n), v("P4", h0, h0 + n), v("T2", h0, h0 + n), ALU.min)
-            send(e + 1, h0, h0 + n)
+        def steps(k, h0, n):
+            kk = KK[k]
+            t1, t2 = v("T1", h0, h0 + n), v("T2", h0, h0 + n)
 
+            def gaps():
+                for q in range(3):
+                    tt(v("P4", h0 + q, h0 + n, 3), v(kk, q, n, 3), v("RUN", h0 + 2, h0 + n, 3), ALU.subtract)
+            return [lambda: scan(v("RUN", h0, h0 + n), v("RST", h0, h0 + n), v(kk, 0, n), 0.0, ALU.max, ALU.min),
+                    lambda: tt(t1, v(SU[k], 0, n), own(e, h0, h0 + n), ALU.min),
+                    gaps,
+                    lambda: tt(t2, v(UU[k], n, 2 * n), t1, ALU.min),
+                    lambda: tt(own(e + 1, h0, h0 + n), v("P4", h0, h0 + n), t2, ALU.min)]
+
+        parts = []
+        done = False
         h = 0
         for k, ch in enumerate(R0_PLAN):
             h0, n = h, sum(sum(x) for x in ch)
@@ -295,46 +310,56 @@ def rank_program(g, core, T, topo):
                 for w in grp:
                     pair(win, "L0", h // 2, V // 2 + h // 2, w // 2, 8 * h, ALU.min)
                     h += w
-                    if pending[0] is not None:
-                        post(*pending[0])
-                        pending[0] = None
+                    if k == 1 and not done:
+                        x = steps(*parts[0])
+                        for i in (0, 1, 2, 3, 4):
+                            x[i]()
+                        send(e + 1, 0, parts[0][2])
+                        done = True
                 last = gi == len(ch) - 1
                 for m in range(8):
-                    mm(v("P%d" % (2 + k), a - h0, h - h0), "mGp", v("MN", 8 * a + m, 8 * h, 8), False, last and m == 7)
+                    mm(v(KK[k], a - h0, h - h0), "mGp", v("MN", 8 * a + m, 8 * h, 8), False, last and m == 7)
                 for m in range(8):
-                    mm(v("P%d" % k, a - h0, h - h0), "mI8", v("MN", 8 * a + m, 8 * h, 8), False, False)
+                    mm(v(SU[k], a - h0, h - h0), "mI8", v("MN", 8 * a + m, 8 * h, 8), False,
+                       last and m == 7 and UU[k] != SU[k])
                 for m in range(8):
-                    mm(v("P%d" % k, n + a - h0, n + h - h0), "mS32", v("MN", 8 * a + m, 8 * h, 8), False, last and m == 7)
-            pending[0] = (k, h0, n)
-        post(*pending[0])
-        arrive(e + 1, len(R0_PLAN))
+                    mm(v(UU[k], n + a - h0, n + h - h0), "mS32", v("MN", 8 * a + m, 8 * h, 8), False, last and m == 7)
+            parts.append((k, h0, n))
+        b, c = steps(*parts[1]), steps(*parts[2])
+        for x in (b[0], b[1], b[2], b[3], c[0], b[4], c[2], c[1], c[3], c[4]):
+            x()
+        send(e + 1, parts[1][1], V)
+        arrive(e + 1, 2)
 
     def prep_round1(ps):
         tt(f("DL"), f("BD1"), v("P4", 0, V, 3), ALU.subtract)
-        tt(f("DW"), v("RUN", 1, V, 3), v("RUN", 2, V, 3), ALU.subtract)
+        tt(f("DH"), v("P4", 2, V, 3), f("BD2"), ALU.min)
         act(f("GS"), v("P4", 0, V))
         scan(v("SC", 0, NB), f("BD0"), f("DL"), 0.0, ALU.max, ALU.max)
-        tt(f("DH"), f("BD2"), f("DW"), ALU.subtract)
         scan(v("SC", NB, 2 * NB), f("BE1"), f("DH"), 0.0, ALU.max, ALU.max)
         cp(f("WO"), v("SC", 15, 256, 16))
         cp(f("TS"), ind(f("TF"), f("WO")))
         act(v("P4", 0, V), f("GS"), ACT.Identity, bias=H, scale=-2.0)
         act(f("SG1"), v("GS", 0, V, 3), ACT.Sign, bias=1.0, scale=-1.0)
         if ps:
-            act(f("OL"), ind(f("OFF"), v("WO", 0, 8)), ACT.Identity, scale=-1.0)
-            act(f("OH"), ind(f("OFF"), v("WO", 8, 16)))
-        permute("TS", 256, None)
-        tt(f("CSH"), v("P4", 0, V), f("CS"), ALU.max)
-        tt(f("LM"), f("BD0"), f("DL"), ALU.max)
+            act(f("OL"), ind(f("COX"), v("WO", 0, 8)), ACT.Identity, scale=-1.0)
+            act(f("OH"), ind(f("COX"), v("WO", 8, 16)))
+        permute("TS", 256)
+        tt(v("SM", 0, 8), v("SC", 15, NB, 16), v("SC", NB + 15, 256, 16), ALU.add)
         tt(f("HH"), f("BE1"), f("DH"), ALU.max)
+        tt(v("SM", 8, 16), f("CB"), v("SM", 0, 8), ALU.subtract)
+        tt(f("CSH"), v("P4", 0, V), f("CS"), ALU.max)
+        ts(f("WB"), v("SM", 8, 16), 3.0, ALU.add)
+        if ps:
+            ts(f("WB1"), v("SM", 12, 16), 3.0 - V // 2, ALU.add)
+        tt(f("LM"), f("BD0"), f("DL"), ALU.max)
         cp(f("L1"), v("P7", 0, 256))
         for k, (b0, b1) in enumerate(R1_CHUNKS):
             d = v("P%d" % (5 + k), b0, b1)
+            mm(d, "mI", v("CK", b0, b1), True, False)
             if ps:
-                mm(d, "mI", v("OL", b0, b1), True, False)
+                mm(d, "mI", v("OL", b0, b1), False, False)
                 mm(d, "mI", v("OH", b0, b1), False, False)
-            else:
-                mm(d, "mI", v("CK", b0, b1), True, False)
 
     def round1(e):
         win = "W%d" % e
@@ -353,32 +378,32 @@ def rank_program(g, core, T, topo):
 
         for k, (b0, b1) in enumerate(R1_CHUNKS):
             for side in (0, 1):
-                for a in range(b0, b1, 64):
-                    sizes = (24, 40) if first[0] else (32, 32)
-                    b = a
-                    for w in sizes:
-                        c = 64 * side + b // 2
-                        pair(win, "L1", c, 128 + c, w // 2, 16 * c, ALU.min)
-                        b += w
-                        if pending[0] is not None:
-                            post(*pending[0])
-                            pending[0] = None
-                    last = side == 1 and a + 64 == b1
-                    base = 1024 * side
-                    for m in range(8):
-                        mm(v("P%d" % (5 + k), a, a + 64), "mGp" if side else "mGn",
-                           v("MN", base + 8 * a + m, base + 8 * a + 512, 8), False, last and m == 7)
+                b = b0
+                for w in R1_PIECES[k][side]:
+                    c = 64 * side + b // 2
+                    pair(win, "L1", c, 128 + c, w // 2, 16 * c, ALU.min)
+                    b += w
+                    if pending[0] is not None:
+                        post(*pending[0])
+                        pending[0] = None
+                base = 1024 * side
+                for m in range(8):
+                    mm(v("P%d" % (5 + k), b0, b1), "mGp" if side else "mGn",
+                       v("MN", base + 8 * b0 + m, base + 8 * b1, 8), False, side == 1 and m == 7)
             pending[0] = (k, b0, b1)
         post(*pending[0])
         arrive(e + 1, len(R1_CHUNKS))
 
     def prep_level(wo, lst, need_z):
-        cp(f(wo), v("SC", 15, NB, 16))
-        cp(v("TS", 0, NB), ind(f("TF"), f(wo)))
+        if lst == "L2":
+            cp(f(wo), v("SC", 15, NB, 16))
+            cp(v("TS", 0, NB), ind(f("TF"), f(wo)))
+            permute("TS", NB)
+            cp(f("TB"), ind(f("TF"), f("WB")))
+        cp(f(lst), v("P7", 0, NB))
         act(f("NCS"), ind(f("CS"), f(wo)), ACT.Identity, scale=-1.0)
         if need_z:
             act(f("C64"), f("NCS"), ACT.Identity, scale=-64.0)
-        permute("TS", NB, lst)
         for k in range(4):
             mm(v("P%d" % k, 0, 256), "mI", f("CM"), True, False)
             for m in range(8):
@@ -386,9 +411,12 @@ def rank_program(g, core, T, topo):
         if need_z:
             mm(v("P5", 0, NB), "mI", f("C64"), True, False)
         mm(v("P6", 0, NB), "mI", f("CX"), True, False)
+        if lst == "L2":
+            permute("TB", NB)
 
     def level(e, lst, need_z):
         w = v("W%d" % e, 0, W)
+        pieces = ((0, 8), (8, 16), (16, 32), (32, 48), (48, 64))
 
         def q(name, k):
             return v(name, 256 * k, 256 * k + 256)
@@ -396,10 +424,12 @@ def rank_program(g, core, T, topo):
         def e_(k):
             return v("P%d" % k, 0, 256)
 
-        def ga(a, b, fn=act):
-            fn(v("GA", 16 * a, 16 * b), ind(w, v(lst, a, b)))
+        def ga(k):
+            a, b = pieces[k]
+            (act if k else cp)(v("GA", 16 * a, 16 * b), ind(w, v(lst, a, b)))
 
-        def s(a, b):
+        def s(k):
+            a, b = pieces[k]
             tt(v("MN", 16 * a, 16 * b), ind(w, v(lst, 64 + a, 64 + b)), v("GA", 16 * a, 16 * b), ALU.add)
             if b % 16 == 0:
                 mm(e_(b // 16 - 1), "mI", q("MN", b // 16 - 1), False, True)
@@ -421,36 +451,16 @@ def rank_program(g, core, T, topo):
             for m in range(8):
                 mm(v(bank, 64 * h, 64 * h + 64), mat, v(src, 512 * h + m, 512 * h + 512, 8), False, stop and m == 7)
 
-        ga(0, 8, cp)
-        ga(8, 16)
-        ga(16, 32)
-        ga(32, 48)
-        s(0, 8)
-        s(8, 16)
-        s(16, 32)
-        r(0)
-        ga(48, 64)
-        s(32, 48)
-        d(0)
-        r(1)
-        s(48, 64)
-        r(2)
-        ab(0)
-        d(1)
-        r(3)
-        if need_z:
-            summ("P5", "mMx", "DD", 0)
-        vv(0)
-        d(2)
-        ab(1)
-        summ("P6", "mGp", "F2", 0)
-        d(3)
-        ab(2)
-        if need_z:
-            summ("P5", "mMx", "DD", 1, True)
-        vv(1)
-        ab(3)
-        summ("P6", "mGp", "F2", 1, True)
+        def zz(h):
+            if need_z:
+                summ("P5", "mMx", "DD", h, h == 1)
+
+        def xx(h):
+            summ("P6", "mGp", "F2", h, h == 1)
+
+        calls_ = {"g": ga, "s": s, "r": r, "d": d, "a": ab, "v": vv, "z": zz, "x": xx}
+        for step in ORDER.split():
+            calls_[step[0]](int(step[1]))
 
     Z, X = v("P5", 0, NB), v("P6", 0, NB)
 
@@ -470,47 +480,48 @@ def rank_program(g, core, T, topo):
         act(own(e + 3), own(e + 2))
         if ps == 0:
             cp(v("COL", 2, 3), v("THI", 0, 1))
-            act(f("AS1"), ind(own(0), f("WA")))
-            act(own(4), own(0))
             ts(f("mGt"), f("fG"), v("COL", 2, 3), ALU.mult, -1.0, ALU.mult)
-        else:
-            act(f("CU1"), ind(f("PF"), f("WA")))
-        tt(f("D1"), f("BD1"), v("GS", 1, V, 3), ALU.subtract)
-        tt(f("D2"), f("BD2"), v("GS", 2, V, 3), ALU.subtract)
-        tt(f("D1"), f("D1"), f("D2"), ALU.max)
-        scan(v("SC", 0, NB), f("BD0"), f("D1"), 0.0, ALU.max, ALU.max)
         level(e + 2, "L2", True)
         new_phase("ZI", "YI", 127)
         ts(v("P6", NB, 2 * NB), X, H, ALU.min, -127.0, ALU.max)
         tt(f("VAL"), v("P6", NB, 2 * NB), f("YI"), ALU.add)
+        if ps == 0:
+            act(f("AS1"), ind(own(0), f("WA")))
+            act(own(4), own(0))
+            act(f("OC1"), ind(f("OFC"), f("WA")))
+        else:
+            act(f("CU1"), ind(f("PF"), f("WA")))
+            act(f("LEV"), f("GS"), ACT.Sign)
+            act(f("LEV"), f("LEV"), ACT.Identity, scale=2.0)
         cp(ind(own(e + 3), f("WA")), f("VAL"))
         send(e + 3, 0, V)
         arrive(e + 3, 1)
         ts(f("AC1"), X, 0.0, ALU.is_le)
         if ps:
             cp(f("ZJ"), Z)
+        else:
+            ts(f("RJ1"), X, 0.0, ALU.is_gt)
         prep_level("WB", "L3", ps == 1)
         if ps == 0:
             act(f("AS0"), ind(own(0), f("WB")))
+            act(f("OC0"), ind(f("OFC"), f("WB")))
             tt(ind(own(4), f("WA")), f("AS1"), f("AC1"), ALU.mult)
-            cp(ind(f("ACC"), f("WA")), f("AC1"))
+            tt(ind(f("COX"), f("WA")), f("OC1"), f("RJ1"), ALU.mult)
             level(e + 3, "L3", False)
             ts(f("AC0"), X, 0.0, ALU.is_le)
             tt(ind(own(4), f("WB")), f("AS0"), f("AC0"), ALU.mult)
             send(4, 0, V)
             arrive(4, 1)
-            cp(ind(f("ACC"), f("WB")), f("AC0"))
-            tt(f("T1"), f("ACC"), f("DOF"), ALU.mult)
-            tt(f("OFF"), f("T1"), f("OFC"), ALU.add)
-            r0_init()
+            ts(f("RJ0"), X, 0.0, ALU.is_gt)
+            tt(ind(f("COX"), f("WB")), f("OC0"), f("RJ0"), ALU.mult)
+            r0_init(1)
         else:
             act(f("CU0"), ind(f("PF"), f("WB")))
             act(v("P4", 0, NB), f("CU0"))
-            ts(f("LEV"), f("GS"), 2.0, ALU.min)
             ts(f("YJ"), f("ZJ"), 6, ALU.arith_shift_right, 255, ALU.bitwise_and)
             cp(ind(f("LEV"), f("WA")), f("ONE"))
-            tt(f("DT"), f("YJ"), f("CU1"), ALU.subtract)
             add("S", lambda: g.sync.dma_start(T.ylev[:], T.LEV[0:128:16, :]), [f("LEV")], [], sem="stL")
+            tt(f("DT"), f("YJ"), f("CU1"), ALU.subtract)
             tt(f("DE"), f("DT"), f("AC1"), ALU.mult)
             tt(ind(f("PF"), f("WA")), f("DE"), f("CU1"), ALU.add)
             level(e + 3, "L3", True)
@@ -518,8 +529,11 @@ def rank_program(g, core, T, topo):
             tt(f("DT"), f("YI"), v("P4", 0, NB), ALU.subtract)
             ts(v("P6", NB, 2 * NB), X, 0.0, ALU.is_le)
             tt(f("DE"), v("P6", NB, 2 * NB), f("DT"), ALU.mult)
-            tt(ind(f("PF"), f("WB")), f("DE"), f("CU0"), ALU.add)
-            add("S", lambda: g.sync.dma_start(T.yphi[:], T.PF[:]), [f("PF")], [], sem="stP")
+            hv = V // 2
+            tt(ind(v("PF", 0, hv), v("WB", 0, 4)), v("DE", 0, 64), v("CU0", 0, 64), ALU.add)
+            add("S", lambda: g.sync.dma_start(T.yphi[:, 0:hv], T.PF[:, 0:hv]), [v("PF", 0, hv)], [], sem="stP0")
+            tt(ind(v("PF", hv, V), f("WB1")), v("DE", 64, NB), v("CU0", 64, NB), ALU.add)
+            add("A", lambda: g.scalar.dma_start(T.yphi[:, hv:V], T.PF[:, hv:V]), [v("PF", hv, V)], [], sem="stP1")
 
     n = {q: 0 for q in queues}
     for op in ops:
@@ -541,4 +555,5 @@ def rank_program(g, core, T, topo):
             ins.then_inc(T.sem["c" + op["q"]], 1)
     g.wait_ge(T.sem.sent, sent[0])
     g.sync.wait_ge(T.sem.stL, 16)
-    g.sync.wait_ge(T.sem.stP, 16)
+    g.sync.wait_ge(T.sem.stP0, 16)
+    g.sync.wait_ge(T.sem.stP1, 16)

@@ -7,12 +7,21 @@ M = 49152.0
 KS = 4 * H
 CO = 2.0 ** 59
 BIG = 1e20
+KEPT = ((1, 2), (0, 2), (0, 1))
 
-R0_PLAN = [[[24, 40], [32, 32], [32, 24], [32, 24]], [[72]], [[40, 32]]]
-SU, UU, KK = ("P0", "P1", "P5"), ("P0", "P1", "P7"), ("P2", "P3", "P6")
+R0_A = (0, 24, 64, 112, 176, 240, 312, 384)
+R0_V = (0, 24, 64, 112, 176, 240, 276, 312, 348, 384)
+R0_G = (0, 64, 112, 176, 240, 312, 384)
+R0_P = (0, 240, 312, 384)
+R0_TAIL = {6: "c0 u0 y0 w0 o0 x0", 8: "c1 u1 y1 w1 c2 o1 y2 u2 w2 o2 x1"}
 R1_CHUNKS = [(0, 80), (80, 128)]
-R1_PIECES = [[(24, 28, 28), (40, 40)], [(48,), (48,)]]
-ORDER = "g0 g1 g2 g3 s0 s1 s2 r0 g4 s3 d0 r1 s4 r2 a0 d1 r3 z0 v0 d2 a1 x0 d3 a2 z1 v1 a3 x1"
+R1_A = (0, 12, 26, 40, 60, 80, 104, 128)
+R1_V = (0, 12, 26, 40, 60, 80, 104, 128)
+R1_G = (0, 40, 80, 128)
+R1_POST = 5
+LV = (0, 8, 16, 32, 48, 64)
+ORDER = "g1 g2 g0 g3 s0 g4 s1 r0 s2 s3 r1 s4 r2 r3 d0 v0 a0 v1 d1 b0 a1 d2 d3 z0 a2 b1 a3 z1 x0 b2 x1"
+PF_A, PF_V = ((0, 64), (64, 88)), ((88, 128),)
 
 SCRATCH = {}
 
@@ -24,25 +33,23 @@ def _sb(names, cols, dtype):
 
 _sb("AI TI PI T2", V, "int32")
 _sb("THI IP IQ", 4, "int32")
-_sb("ZI YI ZJ YJ", NB, "int32")
-_sb("W0 W1 W2 W3 W4 W5 W6 W7 GA MN", W, "bfloat16")
+_sb("ZI YI ZJ YJ ALT", NB, "int32")
+_sb("W0 W1 W4 W5 GA MN", W, "bfloat16")
+_sb("W2 W6", W + N * NB, "bfloat16")
+_sb("DG", 16 * NB, "bfloat16")
 _sb("VV NR F2 DD", 1024, "bfloat16")
-_sb("CSU", 512, "bfloat16")
-_sb("CM", 256, "bfloat16")
-_sb("CS CSH OFF OFC COX", V, "bfloat16")
-_sb("mI mI8 mS32 mGp mGn mGt mMx CK CX NCS C64 VAL AS0 AS1 AC0 AC1 OL OH OC0 OC1 RJ0 RJ1", NB, "bfloat16")
-_sb("TF PF RUN RST T1 GS LEV QF", V, "float32")
-_sb("J1 J2 J3 J4 fI fS fG pA0 pA1 pB0 pB1 B3 BD0 BD1 BD2 BE1 DL DH LM HH D1 SG1 CU0 CU1 DT DE ONE TB",
-    NB, "float32")
-_sb("SC TS", 256, "float32")
+_sb("PRE CSU", 512, "bfloat16")
+_sb("CM NCS C64 AS OC", 256, "bfloat16")
+_sb("CS CSH OFC COX DCX", V, "bfloat16")
+_sb("mI mI8 mS32 mGp mGn mGt mMx CK CX AC0 AC1 OL RJ0 RJ1", NB, "bfloat16")
+_sb("TF PF RUN RST T1 LEV TA TC", V, "float32")
+_sb("J1 J2 J3 J4 fI fS fG pA0 pA1 pB0 pB1 B3 BD0 BD1 BD2 BE1 DL LM HH D1 SG1 DT DE TB LF ALF SC TS", NB, "float32")
+_sb("CU", 256, "float32")
 _sb("COL", 4, "float32")
-_sb("SM", 16, "float32")
-_sb("CB", 8, "float32")
 _sb("L0", V, "uint16")
 _sb("L1", 256, "uint16")
-_sb("L2 L3", NB, "uint16")
-_sb("WO", 16, "uint16")
-_sb("WA WB", 8, "uint16")
+_sb("L2 L3 L4", NB, "uint16")
+_sb("WX", 16, "uint16")
 _sb("WB1", 4, "uint16")
 for _i in range(8):
     SCRATCH["P%d" % _i] = ("psum", [128, 512], "float32")
@@ -154,7 +161,7 @@ def rank_program(g, core, T, topo):
         add("A", lambda: g.scalar.activation(out[0], a[0], func, **kw), [a], [out])
 
     def mm(out, mat, rhs, start, stop):
-        m = v(mat, 0, NB)
+        m = mat if isinstance(mat, tuple) else v(mat, 0, NB)
         add("P", lambda: g.tensor.matmul(out[0], m[0], rhs[0], start, stop), [m, rhs], [out])
 
     def iota(out, pattern, base, cm, flt=True):
@@ -172,9 +179,7 @@ def rank_program(g, core, T, topo):
     mask_near = sum(1 << e for e in eng[1::2])
     sent = [0]
 
-    def send(e, a, b):
-        src = v("W%d" % e, o0 + a, o0 + b)
-
+    def send(e, src):
         def fn():
             trs = []
             for dsts, mask in ((far, mask_far), (near, mask_near)):
@@ -185,8 +190,8 @@ def rank_program(g, core, T, topo):
         add("G", fn, [src], [])
         sent[0] += 2 * half
 
-    def arrive(e, pieces):
-        w = [v("W%d" % e, a, b) for a, b in ((0, o0), (o0 + V, W)) if b > a]
+    def arrive(e, pieces, win, base, n):
+        w = [v(win, base + a, base + b) for a, b in ((0, rank * n), (rank * n + n, N * n)) if b > a]
         add(None, None, [], w, sem="arr%d" % e, total=(N - 1) * half * pieces)
 
     def own(e, a=0, b=V, st=1):
@@ -201,172 +206,167 @@ def rank_program(g, core, T, topo):
     iota(f("J4"), [[16, 8], [1000, 2], [2, 8]], 0, -1)
     iota(f("J1"), [[1, 128]], 0, -1)
     iota(v("IP", 0, 1), [[0, 1]], 0, 1, False)
-    ms(f("CSU"), -31.0 / 64)
-    ms(f("CM"), M)
-    for n_, c_ in (("pA0", 0.0), ("pA1", 1000.0), ("pB0", -1.0), ("pB1", 999.0)):
-        ts(f(n_), f("J4"), c_, ALU.is_equal)
-    cp(own(0), f("AI"))
-    send(0, 0, V)
-    arrive(0, 1)
     iota(f("J2"), [[0, 8], [1, 16]], 0, 0)
     iota(f("J3"), [[1, 8], [0, 16]], 0, 0)
-    iota(f("QF"), [[0, 128], [1, 3]], 0, 0)
-    iota(f("B3"), [[3, 128]], 0, 0)
-    iota(v("SM", 0, 8), [[16, 8]], 0, 0)
-    add("G", lambda: g.dma_start(T.THI[:, 0:1], T.th[:], allow_slow_non_contiguous=True), [], [v("THI", 0, 1)], sem="ldH")
-
-    def permute(src, n):
-        h = n // 2
-        for k, x in enumerate("AB"):
-            mm(v("P7", k * h, k * h + h), "p%s0" % x, v(src, 0, n, 2), True, False)
-            mm(v("P7", k * h, k * h + h), "p%s1" % x, v(src, 1, n, 2), False, True)
-
-    def r0_init(ps):
-        h0 = 0
-        for k, ch in enumerate(R0_PLAN):
-            n = sum(sum(x) for x in ch)
-            mm(v(SU[k], 0, 2 * n), "mI", v("CSU", 0, 2 * n), True, False)
-            if UU[k] != SU[k]:
-                mm(v(UU[k], 0, 2 * n), "mI", v("CSU", 0, 2 * n), True, False)
-            mm(v(KK[k], 0, n), "mI", v("OFF", h0, h0 + n), True, False)
-            h0 += n
-        h0 = 0
-        for k, ch in enumerate(R0_PLAN if ps else []):
-            n = sum(sum(x) for x in ch)
-            mm(v(KK[k], 0, n), "mI", v("COX", h0, h0 + n), False, False)
-            h0 += n
-
+    ms(f("CSU"), -31.0 / 64)
+    for n_, c_ in (("pA0", 0.0), ("pA1", 1000.0), ("pB0", -1.0), ("pB1", 999.0)):
+        ts(f(n_), f("J4"), c_, ALU.is_equal)
     ts(f("fI"), f("J1"), 0.0, ALU.is_equal)
-    cp(f("TF"), f("TI"))
-    permute("TF", V)
     ts(v("IQ", 0, 1), v("IP", 0, 1), 15, ALU.bitwise_and)
     ts(v("IQ", 1, 2), v("IP", 0, 1), 4, ALU.arith_shift_right)
-    cp(f("PF"), f("PI"))
+    ms(f("CM"), M)
     cp(v("COL", 0, 2), v("IQ", 0, 2))
+    ms(f("CK"), H)
+    ts(f("fS"), f("J2"), v("COL", 0, 1), ALU.is_equal)
+    ts(f("fG"), f("J3"), v("COL", 1, 2), ALU.is_equal, KS, ALU.mult)
+    cp(own(0), f("AI"))
+    send(0, own(0))
+    arrive(0, 1, "W0", 0, V)
+    iota(f("B3"), [[3, 128]], 0, 0)
+    add("G", lambda: g.dma_start(T.THI[:, 0:1], T.th[:], allow_slow_non_contiguous=True), [], [v("THI", 0, 1)], sem="ldH")
+
+    def permute(src, n, bank="P7"):
+        h = n // 2
+        for k, x in enumerate("AB"):
+            mm(v(bank, k * h, k * h + h), "p%s0" % x, v(src, 0, n, 2), True, False)
+            mm(v(bank, k * h, k * h + h), "p%s1" % x, v(src, 1, n, 2), False, True)
+
+    prt = list(zip(R0_P, R0_P[1:]))
+
+    def sums(k):
+        n = prt[k][1] - prt[k][0]
+        return ((("P0", 0), ("P0", n), ("P2", 0)), (("P1", 0), ("P1", n), ("P3", 0)),
+                (("P5", 0), ("P7", 0), ("P6", 0)))[k]
+
+    def r0_init(ps, parts=(0, 1, 2)):
+        for k in parts:
+            n = prt[k][1] - prt[k][0]
+            s_, u_, k_ = sums(k)
+            mm(v(s_[0], 0, 2 * n), "mI", v("CSU", 0, 2 * n), True, False)
+            if u_[0] != s_[0]:
+                mm(v(u_[0], 0, n), "mI", v("CSU", 0, n), True, False)
+            mm(v(k_[0], 0, n), "mI", v("PRE", 256, 256 + n), True, False)
+        for k, (a, b) in enumerate(prt if ps else []):
+            mm(v(sums(k)[2][0], 0, b - a), "mI", v("COX", a, b), False, False)
+
+    cp(f("TF"), f("TI"))
+    permute("TF", V)
+    for k, x in enumerate("AB"):
+        for d, (lo, hi) in enumerate(KEPT):
+            mm(v("P%d" % (5 + k), d, V, 3), "p%s0" % x, v("TF", lo, V, 3), True, False)
+            mm(v("P%d" % (5 + k), d, V, 3), "p%s1" % x, v("TF", hi, V, 3), False, True)
+    cp(f("PF"), f("PI"))
     act(f("mI"), f("fI"))
     act(f("mI8"), f("fI"), ACT.Identity, scale=0.125)
     act(f("J1"), f("fI"), ACT.Identity, scale=8.0)
-    act(f("ONE"), f("fI"), ACT.Identity, bias=1.0, scale=0.0)
-    act(f("CK"), f("fI"), ACT.Identity, bias=H, scale=0.0)
-    act(f("CX"), f("fI"), ACT.Identity, bias=-KS / 2, scale=0.0)
-    ts(v("P4", 0, V), f("PF"), 128.0, ALU.is_gt, -256.0, ALU.mult)
-    ts(f("fS"), f("J2"), v("COL", 0, 1), ALU.is_equal)
-    ts(f("fG"), f("J3"), v("COL", 1, 2), ALU.is_equal, KS, ALU.mult)
-    tt(f("CS"), v("P4", 0, V), f("PF"), ALU.add)
-    cp(f("L0"), v("P7", 0, V))
     act(f("mS32"), f("fS"), ACT.Identity, scale=1.0 / 32)
     act(f("mGp"), f("fG"))
-    act(f("J2"), f("fS"), ACT.Identity, bias=-1.0)
-    act(f("OFF"), f("QF"), ACT.Identity, scale=H)
-    r0_init(0)
-    act(f("RST"), f("QF"), ACT.Identity, bias=BIG, scale=-2 * BIG)
     act(f("mGn"), f("fG"), ACT.Identity, scale=-1.0)
-    act(f("OFC"), f("QF"), ACT.Identity, bias=-3 * CO, scale=CO)
-    act(f("COX"), f("QF"), ACT.Identity, scale=0.0)
-    tt(f("mMx"), f("J1"), f("fS"), ALU.add)
+    act(f("J2"), f("fS"), ACT.Identity, bias=-1.0)
+    for q in range(3):
+        ms(v("PRE", 256 + q, 512, 3), q * H)
+        ms(v("OFC", q, V, 3), (q - 3) * CO)
+    ts(v("P4", 0, V), f("PF"), 128.0, ALU.is_gt, -256.0, ALU.mult)
+    ms(f("RST"), -BIG)
+    tt(f("CS"), v("P4", 0, V), f("PF"), ALU.add)
+    cp(f("L0"), v("P7", 0, V))
+    ms(v("RST", 0, V, 3), BIG)
+    ms(f("CX"), -KS / 2)
+    ms(f("COX"), 0.0)
+    r0_init(0, (0, 1))
+    act(f("TA"), v("P5", 0, V))
+    for s_ in range(16):
+        ts(v("DG", NB * s_, NB * s_ + NB), f("mI"), v("fS", s_, s_ + 1), ALU.mult, -8192.0, ALU.mult)
     tt(f("BD0"), f("B3"), f("fS"), ALU.mult)
-    ts(f("CB"), v("SM", 0, 8), v("COL", 0, 1), ALU.add, 9.0, ALU.mult)
+    tt(f("mMx"), f("J1"), f("fS"), ALU.add)
     tt(f("BE1"), f("BD0"), f("fS"), ALU.add)
     tt(f("BD1"), f("BE1"), f("J2"), ALU.add)
     tt(f("BD2"), f("BD1"), f("fS"), ALU.add)
 
-    first = [True]
-
-    def pair(win, lst, la, lb, cols, pos, op):
-        n = 16 * cols
-        ga = v("GA", pos, pos + n)
-        w = v(win, 0, W)
-        if first[0]:
-            cp(ga, ind(w, v(lst, la, la + cols)))
-            first[0] = False
-        else:
-            act(ga, ind(w, v(lst, la, la + cols)))
-        tt(v("MN", pos, pos + n), ind(w, v(lst, lb, lb + cols)), ga, op)
+    WA, WB = v("WX", 0, 8), v("WX", 8, 16)
 
     def round0(e):
-        win = "W%d" % e
-        first[0] = True
+        w = v("W%d" % e, 0, W)
 
-        def steps(k, h0, n):
-            kk = KK[k]
-            t1, t2 = v("T1", h0, h0 + n), v("T2", h0, h0 + n)
+        def direct(a, b):
+            k = [j for j, (x, y) in enumerate(prt) if x <= a < y][0]
+            s_, u_, k_ = sums(k)
+            o = a - prt[k][0]
+            for x, mat in ((k_, "mGp"), (s_, "mI8"), (u_, "mS32")):
+                for m in range(8):
+                    mm(v(x[0], x[1] + o, x[1] + o + b - a), mat, v("MN", 8 * a + m, 8 * b, 8), False,
+                       m == 7 and b == prt[k][1] and not (x is s_ and s_[0] == u_[0]))
 
-            def gaps():
-                for q in range(3):
-                    tt(v("P4", h0 + q, h0 + n, 3), v(kk, q, n, 3), v("RUN", h0 + 2, h0 + n, 3), ALU.subtract)
-            return [lambda: scan(v("RUN", h0, h0 + n), v("RST", h0, h0 + n), v(kk, 0, n), 0.0, ALU.max, ALU.min),
-                    lambda: tt(t1, v(SU[k], 0, n), own(e, h0, h0 + n), ALU.min),
-                    gaps,
-                    lambda: tt(t2, v(UU[k], n, 2 * n), t1, ALU.min),
-                    lambda: tt(own(e + 1, h0, h0 + n), v("P4", h0, h0 + n), t2, ALU.min)]
+        def at(x, k, q=0, st=1):
+            return v(x[0], x[1] + q, x[1] + prt[k][1] - prt[k][0], st)
 
-        parts = []
-        done = False
-        h = 0
-        for k, ch in enumerate(R0_PLAN):
-            h0, n = h, sum(sum(x) for x in ch)
-            for gi, grp in enumerate(ch):
-                a = h
-                for w in grp:
-                    pair(win, "L0", h // 2, V // 2 + h // 2, w // 2, 8 * h, ALU.min)
-                    h += w
-                    if k == 1 and not done:
-                        x = steps(*parts[0])
-                        for i in (0, 1, 2, 3, 4):
-                            x[i]()
-                        send(e + 1, 0, parts[0][2])
-                        done = True
-                last = gi == len(ch) - 1
-                for m in range(8):
-                    mm(v(KK[k], a - h0, h - h0), "mGp", v("MN", 8 * a + m, 8 * h, 8), False, last and m == 7)
-                for m in range(8):
-                    mm(v(SU[k], a - h0, h - h0), "mI8", v("MN", 8 * a + m, 8 * h, 8), False,
-                       last and m == 7 and UU[k] != SU[k])
-                for m in range(8):
-                    mm(v(UU[k], n + a - h0, n + h - h0), "mS32", v("MN", 8 * a + m, 8 * h, 8), False, last and m == 7)
-            parts.append((k, h0, n))
-        b, c = steps(*parts[1]), steps(*parts[2])
-        for x in (b[0], b[1], b[2], b[3], c[0], b[4], c[2], c[1], c[3], c[4]):
-            x()
-        send(e + 1, parts[1][1], V)
-        arrive(e + 1, 2)
+        def sc(k):
+            scan(v("RUN", *prt[k]), v("RST", *prt[k]), at(sums(k)[2], k), 0.0, ALU.max, ALU.min)
+
+        def gaps(k):
+            a, b = prt[k]
+            for q in range(3):
+                tt(v("P4", a + q, b, 3), at(sums(k)[2], k, q, 3), v("RUN", a + 2, b, 3), ALU.subtract)
+
+        def t1(k):
+            tt(v("T1", *prt[k]), at(sums(k)[0], k), own(e, *prt[k]), ALU.min)
+
+        def t2(k):
+            tt(v("T2", *prt[k]), at(sums(k)[1], k), v("T1", *prt[k]), ALU.min)
+
+        def out(k):
+            tt(own(e + 1, *prt[k]), v("P4", *prt[k]), v("T2", *prt[k]), ALU.min)
+
+        def xs(k):
+            send(e + 1, own(e + 1, prt[1][0], V) if k else own(e + 1, *prt[0]))
+
+        steps = {"c": sc, "y": gaps, "u": t1, "w": t2, "o": out, "x": xs}
+        for a, b in zip(R0_A, R0_A[1:]):
+            (act if a else cp)(v("GA", 8 * a, 8 * b), ind(w, v("L0", a // 2, b // 2)))
+        if e == 0:
+            act(f("TC"), v("P6", 0, V))
+            act(own(4), own(0))
+        for i, (a, b) in enumerate(zip(R0_V, R0_V[1:])):
+            tt(v("MN", 8 * a, 8 * b), ind(w, v("L0", (V + a) // 2, (V + b) // 2)), v("GA", 8 * a, 8 * b), ALU.min)
+            if b in R0_G:
+                direct(R0_G[R0_G.index(b) - 1], b)
+            if b == R0_P[2] and e == 0:
+                r0_init(0, (2,))
+            for step in R0_TAIL.get(i, "").split():
+                steps[step[0]](int(step[1]))
+        arrive(e + 1, 2, "W%d" % (e + 1), 0, V)
 
     def prep_round1(ps):
-        tt(f("DL"), f("BD1"), v("P4", 0, V, 3), ALU.subtract)
-        tt(f("DH"), v("P4", 2, V, 3), f("BD2"), ALU.min)
-        act(f("GS"), v("P4", 0, V))
-        scan(v("SC", 0, NB), f("BD0"), f("DL"), 0.0, ALU.max, ALU.max)
-        scan(v("SC", NB, 2 * NB), f("BE1"), f("DH"), 0.0, ALU.max, ALU.max)
-        cp(f("WO"), v("SC", 15, 256, 16))
-        cp(f("TS"), ind(f("TF"), f("WO")))
-        act(v("P4", 0, V), f("GS"), ACT.Identity, bias=H, scale=-2.0)
-        act(f("SG1"), v("GS", 0, V, 3), ACT.Sign, bias=1.0, scale=-1.0)
+        x = v("P7", 0, NB)
+        tt(x, v("P4", 0, V, 3), f("fS"), ALU.min)
+        tt(f("DL"), f("BD2"), v("P4", 2, V, 3), ALU.subtract)
+        tt(f("D1"), x, f("BD0"), ALU.add)
+        tt(v("P7", NB, 2 * NB), v("P4", 2, V, 3), f("BD2"), ALU.min)
+        scan(f("SC"), f("DL"), f("D1"), 0.0, ALU.max, ALU.max)
+        act(f("SG1"), v("P4", 0, V, 3), ACT.Sign, bias=1.0, scale=-1.0)
+        act(v("P4", 0, V), v("P4", 0, V), ACT.Identity, bias=3 * H, scale=-4.0)
+        tt(f("LM"), f("BD1"), x, ALU.subtract)
+        cp(WB, v("SC", 15, NB, 16))
+        tt(f("HH"), v("P7", NB, 2 * NB), f("BE1"), ALU.max)
+        cp(v("L1", 0, NB), ind(f("TA"), WB))
+        cp(v("L1", NB, 256), ind(f("TC"), WB))
         if ps:
-            act(f("OL"), ind(f("COX"), v("WO", 0, 8)), ACT.Identity, scale=-1.0)
-            act(f("OH"), ind(f("COX"), v("WO", 8, 16)))
-        permute("TS", 256)
-        tt(v("SM", 0, 8), v("SC", 15, NB, 16), v("SC", NB + 15, 256, 16), ALU.add)
-        tt(f("HH"), f("BE1"), f("DH"), ALU.max)
-        tt(v("SM", 8, 16), f("CB"), v("SM", 0, 8), ALU.subtract)
+            act(f("OL"), ind(f("DCX"), WB))
+            ts(f("WB1"), v("SC", 79, NB, 16), -(V // 2) * 1.0, ALU.add)
+        act(f("TB"), ind(f("TF"), WB))
         tt(f("CSH"), v("P4", 0, V), f("CS"), ALU.max)
-        ts(f("WB"), v("SM", 8, 16), 3.0, ALU.add)
-        if ps:
-            ts(f("WB1"), v("SM", 12, 16), 3.0 - V // 2, ALU.add)
-        tt(f("LM"), f("BD0"), f("DL"), ALU.max)
-        cp(f("L1"), v("P7", 0, 256))
         for k, (b0, b1) in enumerate(R1_CHUNKS):
             d = v("P%d" % (5 + k), b0, b1)
             mm(d, "mI", v("CK", b0, b1), True, False)
             if ps:
                 mm(d, "mI", v("OL", b0, b1), False, False)
-                mm(d, "mI", v("OH", b0, b1), False, False)
+        permute("TB", NB, "P4")
 
     def round1(e):
-        win = "W%d" % e
-        first[0] = True
-        pending = [None]
+        w = v("W%d" % e, 0, W)
 
-        def post(k, b0, b1):
+        def post(k):
+            b0, b1 = R1_CHUNKS[k]
             p = "P%d" % (5 + k)
             E, F, Y = v(p, 128 + b0, 128 + b1), v(p, 256 + b0, 256 + b1), v(p, 384 + b0, 384 + b1)
             ts(E, v(p, b0, b1), H, ALU.min, -H, ALU.max)
@@ -374,49 +374,84 @@ def rank_program(g, core, T, topo):
             tt(Y, E, v("SG1", b0, b1), ALU.mult)
             for q, x in ((0, E), (2, F), (1, Y)):
                 tt(own(e + 1, 3 * b0 + q, 3 * b1, 3), x, v("CSH", 3 * b0 + q, 3 * b1, 3), ALU.max)
-            send(e + 1, 3 * b0, 3 * b1)
+            send(e + 1, own(e + 1, 3 * b0, 3 * b1))
 
-        for k, (b0, b1) in enumerate(R1_CHUNKS):
-            for side in (0, 1):
-                b = b0
-                for w in R1_PIECES[k][side]:
-                    c = 64 * side + b // 2
-                    pair(win, "L1", c, 128 + c, w // 2, 16 * c, ALU.min)
-                    b += w
-                    if pending[0] is not None:
-                        post(*pending[0])
-                        pending[0] = None
-                base = 1024 * side
+        for a, b in zip(R1_A, R1_A[1:]):
+            (act if a else cp)(v("GA", 16 * a, 16 * b), ind(w, v("L1", a, b)))
+        act(v("NCS", NB, 256), ind(f("CS"), WB), ACT.Identity, scale=-1.0)
+        act(f("LF"), v("P4", 0, NB))
+        if e == 1:
+            act(v("AS", NB, 256), ind(own(0), WB))
+        else:
+            act(v("C64", NB, 256), v("NCS", NB, 256), ACT.Identity, scale=-64.0)
+            act(v("CU", NB, 256), ind(f("PF"), WB))
+        for i, (a, b) in enumerate(zip(R1_V, R1_V[1:])):
+            tt(v("MN", 16 * a, 16 * b), ind(w, v("L1", NB + a, NB + b)), v("GA", 16 * a, 16 * b), ALU.min)
+            if b in R1_G:
+                a = R1_G[R1_G.index(b) - 1]
+                k = int(a >= R1_CHUNKS[1][0])
+                for m in range(16):
+                    mm(v("P%d" % (5 + k), a, b), "mGp" if m >= 8 else "mGn", v("MN", 16 * a + m, 16 * b, 16), False,
+                       m == 15 and b == R1_CHUNKS[k][1])
+            if i == R1_POST:
+                post(0)
+        post(1)
+        arrive(e + 1, len(R1_CHUNKS), "W%d" % (e + 1), 0, V)
+
+    def fill(o, banks):
+        for k in banks:
+            if k < 4:
+                mm(v("P%d" % k, 0, 256), "mI", f("CM"), True, False)
                 for m in range(8):
-                    mm(v("P%d" % (5 + k), b0, b1), "mGp" if side else "mGn",
-                       v("MN", base + 8 * b0 + m, base + 8 * b1, 8), False, side == 1 and m == 7)
-            pending[0] = (k, b0, b1)
-        post(*pending[0])
-        arrive(e + 1, len(R1_CHUNKS))
+                    mm(v("P%d" % k, m, 256, 8), "mI", v("NCS", o + 32 * k, o + 32 * k + 32), False, False)
+            else:
+                mm(v("P%d" % k, 0, NB), "mI", v("C64", o, o + NB) if k == 5 else f("CX"), True, False)
 
-    def prep_level(wo, lst, need_z):
-        if lst == "L2":
-            cp(f(wo), v("SC", 15, NB, 16))
-            cp(v("TS", 0, NB), ind(f("TF"), f(wo)))
-            permute("TS", NB)
-            cp(f("TB"), ind(f("TF"), f("WB")))
-        cp(f(lst), v("P7", 0, NB))
-        act(f("NCS"), ind(f("CS"), f(wo)), ACT.Identity, scale=-1.0)
-        if need_z:
-            act(f("C64"), f("NCS"), ACT.Identity, scale=-64.0)
-        for k in range(4):
-            mm(v("P%d" % k, 0, 256), "mI", f("CM"), True, False)
-            for m in range(8):
-                mm(v("P%d" % k, m, 256, 8), "mI", v("NCS", 32 * k, 32 * k + 32), False, False)
-        if need_z:
-            mm(v("P5", 0, NB), "mI", f("C64"), True, False)
-        mm(v("P6", 0, NB), "mI", f("CX"), True, False)
-        if lst == "L2":
-            permute("TB", NB)
+    def prep_levels(ps):
+        cp(WA, v("SC", 15, NB, 16))
+        cp(f("TS"), ind(f("TF"), WA))
+        act(v("NCS", 0, NB), ind(f("CS"), WA), ACT.Identity, scale=-1.0)
+        permute("TS", NB)
+        cp(f("L3"), v("P4", 0, NB))
+        ts(f("ALT"), v("P4", 0, NB), 1.0 / 3, ALU.mult, W - 1.0 / 3, ALU.add)
+        if ps == 0:
+            cp(v("COL", 2, 3), v("THI", 0, 1))
+        cp(f("ALF"), f("ALT"))
+        if ps == 0:
+            ts(f("mGt"), f("fG"), v("COL", 2, 3), ALU.mult, -1.0, ALU.mult)
+        cp(f("L2"), v("P7", 0, NB))
+        act(v("C64", 0, NB), v("NCS", 0, NB), ACT.Identity, scale=-64.0)
+        fill(0, (0, 1, 2, 3, 5, 6))
+        if ps == 0:
+            act(v("AS", 0, NB), ind(own(0), WA))
+        else:
+            act(v("CU", 0, NB), ind(f("PF"), WA))
+            act(f("LEV"), own(6), ACT.Relu, bias=2.0, scale=-1.0 / H)
+            act(v("P4", 0, NB), v("CU", NB, 256))
+            add("S", lambda: g.sync.dma_start(T.ylev[:], T.LEV[0:128:16, :]), [f("LEV")], [], sem="stL")
 
-    def level(e, lst, need_z):
-        w = v("W%d" % e, 0, W)
-        pieces = ((0, 8), (8, 16), (16, 32), (32, 48), (48, 64))
+    def look(e, scalar):
+        for a, b in PF_A if scalar else PF_V:
+            x, y = v("GA", 1024 + 16 * a, 1024 + 16 * b), ind(v("W%d" % e, 0, W), v("L3", a, b))
+            if scalar:
+                act(x, y, ACT.Abs, bias=-1.0, scale=1.0 / H)
+            else:
+                ts(x, y, H, ALU.not_equal)
+
+    def turn(h):
+        return v(("P7", "P4")[h], NB, NB + 64)
+
+    def pick(h):
+        mm(turn(h), "fI", v("ALF", 64 * h, 64 * h + 64), True, False)
+        for s_ in range(16):
+            mm(turn(h), v("DG", NB * s_, NB * s_ + NB), v("GA", 1024 * (h + 1) + s_, 1024 * (h + 2), 16), False, s_ == 15)
+
+    def relist(h):
+        tt(turn(h), turn(h), v("LF", 64 * h, 64 * h + 64), ALU.max)
+        cp(v("L4", 64 * h, 64 * h + 64), turn(h))
+
+    def level(w, lst, need_z, aside):
+        pieces = list(zip(LV, LV[1:]))
 
         def q(name, k):
             return v(name, 256 * k, 256 * k + 256)
@@ -458,7 +493,11 @@ def rank_program(g, core, T, topo):
         def xx(h):
             summ("P6", "mGp", "F2", h, h == 1)
 
-        calls_ = {"g": ga, "s": s, "r": r, "d": d, "a": ab, "v": vv, "z": zz, "x": xx}
+        def by(k):
+            if k in aside:
+                aside[k]()
+
+        calls_ = {"g": ga, "s": s, "r": r, "d": d, "a": ab, "v": vv, "z": zz, "x": xx, "b": by}
         for step in ORDER.split():
             calls_[step[0]](int(step[1]))
 
@@ -475,64 +514,55 @@ def rank_program(g, core, T, topo):
         round1(e + 1)
         for k, (b0, b1) in enumerate(R1_CHUNKS):
             tt(v("D1", b0, b1), v("P%d" % (5 + k), 256 + b0, 256 + b1), v("HH", b0, b1), ALU.min)
-        scan(v("SC", 0, NB), f("LM"), f("D1"), 0.0, ALU.max, ALU.max)
-        prep_level("WA", "L2", True)
-        act(own(e + 3), own(e + 2))
-        if ps == 0:
-            cp(v("COL", 2, 3), v("THI", 0, 1))
-            ts(f("mGt"), f("fG"), v("COL", 2, 3), ALU.mult, -1.0, ALU.mult)
-        level(e + 2, "L2", True)
+        scan(f("SC"), f("LM"), f("D1"), 0.0, ALU.max, ALU.max)
+        prep_levels(ps)
+        win = "W%d" % (e + 2)
+        level(v(win, 0, W), "L2", True, {})
+        look(e + 2, True)
         new_phase("ZI", "YI", 127)
-        ts(v("P6", NB, 2 * NB), X, H, ALU.min, -127.0, ALU.max)
-        tt(f("VAL"), v("P6", NB, 2 * NB), f("YI"), ALU.add)
-        if ps == 0:
-            act(f("AS1"), ind(own(0), f("WA")))
-            act(own(4), own(0))
-            act(f("OC1"), ind(f("OFC"), f("WA")))
-        else:
-            act(f("CU1"), ind(f("PF"), f("WA")))
-            act(f("LEV"), f("GS"), ACT.Sign)
-            act(f("LEV"), f("LEV"), ACT.Identity, scale=2.0)
-        cp(ind(own(e + 3), f("WA")), f("VAL"))
-        send(e + 3, 0, V)
-        arrive(e + 3, 1)
-        ts(f("AC1"), X, 0.0, ALU.is_le)
         if ps:
             cp(f("ZJ"), Z)
-        else:
-            ts(f("RJ1"), X, 0.0, ALU.is_gt)
-        prep_level("WB", "L3", ps == 1)
+        ts(v("P6", NB, 2 * NB), X, H, ALU.min, -127.0, ALU.max)
+        val = v(win, W + rank * NB, W + rank * NB + NB)
+        tt(val, v("P6", NB, 2 * NB), f("YI"), ALU.add)
+        send(e + 3, val)
+        arrive(e + 3, 1, win, W, NB)
+        fill(NB, (0, 1))
+        look(e + 2, False)
+        pick(0)
+        pick(1)
+        fill(NB, (2, 3, 5, 6) if ps else (2, 3, 6))
+        ts(f("AC1"), val, 1000.0, ALU.is_lt)
+        relist(0)
+        if ps:
+            ts(f("YJ"), f("ZJ"), 6, ALU.arith_shift_right, 255, ALU.bitwise_and)
+        relist(1)
         if ps == 0:
-            act(f("AS0"), ind(own(0), f("WB")))
-            act(f("OC0"), ind(f("OFC"), f("WB")))
-            tt(ind(own(4), f("WA")), f("AS1"), f("AC1"), ALU.mult)
-            tt(ind(f("COX"), f("WA")), f("OC1"), f("RJ1"), ALU.mult)
-            level(e + 3, "L3", False)
+            level(f(win), "L4", False, {2: lambda: tt(ind(own(4), WA), v("AS", 0, NB), f("AC1"), ALU.mult)})
             ts(f("AC0"), X, 0.0, ALU.is_le)
-            tt(ind(own(4), f("WB")), f("AS0"), f("AC0"), ALU.mult)
-            send(4, 0, V)
-            arrive(4, 1)
+            tt(ind(own(4), WB), v("AS", NB, 256), f("AC0"), ALU.mult)
+            send(4, own(4))
+            arrive(4, 1, "W4", 0, V)
+            act(f("OC"), ind(f("OFC"), f("WX")))
             ts(f("RJ0"), X, 0.0, ALU.is_gt)
-            tt(ind(f("COX"), f("WB")), f("OC0"), f("RJ0"), ALU.mult)
+            ts(f("RJ1"), val, 1000.0, ALU.is_gt)
+            tt(ind(f("COX"), WA), v("OC", 0, NB), f("RJ1"), ALU.mult)
+            tt(ind(f("COX"), WB), v("OC", NB, 256), f("RJ0"), ALU.mult)
+            for d, (lo, hi) in enumerate(KEPT):
+                tt(v("DCX", d, V, 3), v("COX", hi, V, 3), v("COX", lo, V, 3), ALU.subtract)
             r0_init(1)
         else:
-            act(f("CU0"), ind(f("PF"), f("WB")))
-            act(v("P4", 0, NB), f("CU0"))
-            ts(f("YJ"), f("ZJ"), 6, ALU.arith_shift_right, 255, ALU.bitwise_and)
-            cp(ind(f("LEV"), f("WA")), f("ONE"))
-            add("S", lambda: g.sync.dma_start(T.ylev[:], T.LEV[0:128:16, :]), [f("LEV")], [], sem="stL")
-            tt(f("DT"), f("YJ"), f("CU1"), ALU.subtract)
-            tt(f("DE"), f("DT"), f("AC1"), ALU.mult)
-            tt(ind(f("PF"), f("WA")), f("DE"), f("CU1"), ALU.add)
-            level(e + 3, "L3", True)
+            level(f(win), "L4", True, {0: lambda: tt(f("DT"), f("YJ"), v("CU", 0, NB), ALU.subtract),
+                                       1: lambda: tt(f("DE"), f("DT"), f("AC1"), ALU.mult),
+                                       2: lambda: tt(ind(f("PF"), WA), f("DE"), v("CU", 0, NB), ALU.add)})
             new_phase("ZI", "YI", 0)
             tt(f("DT"), f("YI"), v("P4", 0, NB), ALU.subtract)
             ts(v("P6", NB, 2 * NB), X, 0.0, ALU.is_le)
             tt(f("DE"), v("P6", NB, 2 * NB), f("DT"), ALU.mult)
             hv = V // 2
-            tt(ind(v("PF", 0, hv), v("WB", 0, 4)), v("DE", 0, 64), v("CU0", 0, 64), ALU.add)
+            tt(ind(v("PF", 0, hv), v("WX", 8, 12)), v("DE", 0, 64), v("CU", NB, NB + 64), ALU.add)
             add("S", lambda: g.sync.dma_start(T.yphi[:, 0:hv], T.PF[:, 0:hv]), [v("PF", 0, hv)], [], sem="stP0")
-            tt(ind(v("PF", hv, V), f("WB1")), v("DE", 64, NB), v("CU0", 64, NB), ALU.add)
+            tt(ind(v("PF", hv, V), f("WB1")), v("DE", 64, NB), v("CU", NB + 64, 256), ALU.add)
             add("A", lambda: g.scalar.dma_start(T.yphi[:, hv:V], T.PF[:, hv:V]), [v("PF", hv, V)], [], sem="stP1")
 
     n = {q: 0 for q in queues}

from concourse.bass import DstId, RemoteDMATransfer
from concourse.mybir import AluOpType, ActivationFunctionType

N, V, W, NB = 8, 384, 3072, 128
H = 2.0 ** 41
M = 49152.0
KS = 4 * H
CO = 2.0 ** 59
BIG = 1e20
KEPT = ((1, 2), (0, 2), (0, 1))

R0_A = (0, 24, 64, 112, 176, 240, 312, 384)
R0_V = (0, 24, 64, 112, 176, 240, 276, 312, 348, 384)
R0_G = (0, 64, 112, 176, 240, 312, 384)
R0_P = (0, 240, 312, 384)
R0_TAIL = {6: "c0 u0 y0 w0 o0 x0", 8: "c1 u1 y1 w1 c2 o1 y2 u2 w2 o2 x1"}
R1_CHUNKS = [(0, 80), (80, 128)]
R1_A = (0, 12, 26, 40, 60, 80, 104, 128)
R1_V = (0, 12, 26, 40, 60, 80, 104, 128)
R1_G = (0, 40, 80, 128)
R1_POST = 5
LV = (0, 8, 16, 32, 48, 64)
ORDER = "g1 g2 g0 g3 s0 g4 s1 r0 s2 s3 r1 s4 r2 r3 d0 v0 a0 v1 d1 b0 a1 d2 d3 z0 a2 b1 a3 z1 x0 b2 x1"
PF_A, PF_V = ((0, 64), (64, 88)), ((88, 128),)

SCRATCH = {}


def _sb(names, cols, dtype):
    for n in names.split():
        SCRATCH[n] = ("sbuf", [128, cols], dtype)


_sb("AI TI PI T2", V, "int32")
_sb("THI IP IQ", 4, "int32")
_sb("ZI YI ZJ YJ ALT", NB, "int32")
_sb("W0 W1 W4 W5 GA MN", W, "bfloat16")
_sb("W2 W6", W + N * NB, "bfloat16")
_sb("DG", 16 * NB, "bfloat16")
_sb("VV NR F2 DD", 1024, "bfloat16")
_sb("PRE CSU", 512, "bfloat16")
_sb("CM NCS C64 AS OC", 256, "bfloat16")
_sb("CS CSH OFC COX DCX", V, "bfloat16")
_sb("mI mI8 mS32 mGp mGn mGt mMx CK CX AC0 AC1 OL RJ0 RJ1", NB, "bfloat16")
_sb("TF PF RUN RST T1 LEV TA TC", V, "float32")
_sb("J1 J2 J3 J4 fI fS fG pA0 pA1 pB0 pB1 B3 BD0 BD1 BD2 BE1 DL LM HH D1 SG1 DT DE TB LF ALF SC TS", NB, "float32")
_sb("CU", 256, "float32")
_sb("COL", 4, "float32")
_sb("L0", V, "uint16")
_sb("L1", 256, "uint16")
_sb("L2 L3 L4", NB, "uint16")
_sb("WX", 16, "uint16")
_sb("WB1", 4, "uint16")
for _i in range(8):
    SCRATCH["P%d" % _i] = ("psum", [128, 512], "float32")

SEMAPHORES = (["cV", "cA", "cP", "cG", "ldA", "ldT", "ldP", "ldH", "stP0", "stP1", "stL", "sent"]
              + ["arr%d" % i for i in range(8)])

ALU = AluOpType
ACT = ActivationFunctionType


def rank_program(g, core, T, topo):
    rank = T.rank_of(core)
    if rank is None:
        return
    o0 = rank * V
    queues = {"V": g.vector, "A": g.scalar, "P": g.tensor, "G": g, "S": g.sync}
    ops = []
    hist = {}
    known = {q: {} for q in queues}
    count = {q: 0 for q in queues}

    def v(name, a, b, st=1):
        return (T[name][:, a:b:st] if st != 1 else T[name][:, a:b], name, a, b, st, None)

    def ind(win, off):
        return (win[0].indirect(off[0]), win[1], win[2], win[3], 1, off)

    def meet(a, b):
        if a[0] >= b[1] or b[0] >= a[1]:
            return False
        return a[2] != b[2] or (a[0] - b[0]) % a[2] == 0

    def add(q, fn, reads, writes, sem=None, total=16):
        acc = []
        for rs, wr in ((reads, False), (writes, True)):
            for r in rs:
                acc.append((r[1], r[2:5], wr))
                if r[5] is not None:
                    acc.append((r[5][1], r[5][2:5], False))
        op = {"q": q, "fn": fn, "waits": [], "mark": False, "sem": sem, "total": total}
        if sem is None:
            count[q] += 1
            op["key"], op["idx"] = q, count[q]
        else:
            op["key"], op["idx"] = sem, 1
        deps = []
        for (name, rg, wr) in acc:
            psum = SCRATCH[name][0] == "psum"
            for (r2, o2, w2) in hist.get(name, []):
                clash = (wr or w2) and meet(rg, r2)
                if psum:
                    if o2["q"] == q and (q == "P" or not clash):
                        continue
                elif not clash:
                    continue
                deps.append(o2)
        if q is not None:
            kn = known[q]
            deps.sort(key=lambda o: -o["seq"])
            for o2 in deps:
                if kn.get(o2["key"], 0) >= o2["idx"]:
                    continue
                op["waits"].append(o2)
                o2["mark"] = True
                for k, x in o2["clock"].items():
                    if kn.get(k, 0) < x:
                        kn[k] = x
            op["clock"] = dict(kn)
        else:
            op["clock"] = {}
        op["clock"][op["key"]] = op["idx"]
        op["seq"] = len(ops)
        ops.append(op)
        for (name, rg, wr) in acc:
            hist.setdefault(name, []).append((rg, op, wr))
        return op

    def rd(*xs):
        return [x for x in xs if isinstance(x, tuple)]

    def ap(x):
        return x[0] if isinstance(x, tuple) else x

    def tt(out, a, b, op):
        add("V", lambda: g.vector.tensor_tensor(out[0], a[0], b[0], op), [a, b], [out])

    def ts(out, a, s1, op0, s2=None, op1=None):
        if op1 is None:
            add("V", lambda: g.vector.tensor_scalar(out[0], a[0], ap(s1), None, op0), rd(a, s1), [out])
        else:
            add("V", lambda: g.vector.tensor_scalar(out[0], a[0], ap(s1), ap(s2), op0, op1), rd(a, s1, s2), [out])

    def cp(out, a):
        add("V", lambda: g.vector.tensor_copy(out[0], a[0]), [a], [out])

    def ms(out, c):
        add("V", lambda: g.vector.memset(out[0], c), [], [out])

    def scan(out, a, b, init, op0, op1):
        add("V", lambda: g.vector.tensor_tensor_scan(out[0], a[0], b[0], init, op0, op1), [a, b], [out])

    def act(out, a, func=ACT.Copy, bias=None, scale=None):
        kw = {}
        if bias is not None:
            kw["bias"] = bias
        if scale is not None:
            kw["scale"] = scale
        add("A", lambda: g.scalar.activation(out[0], a[0], func, **kw), [a], [out])

    def mm(out, mat, rhs, start, stop):
        m = mat if isinstance(mat, tuple) else v(mat, 0, NB)
        add("P", lambda: g.tensor.matmul(out[0], m[0], rhs[0], start, stop), [m, rhs], [out])

    def iota(out, pattern, base, cm, flt=True):
        if flt:
            add("G", lambda: g.iota(out[0], pattern, base, cm, allow_small_or_imprecise_dtypes=True), [], [out])
        else:
            add("G", lambda: g.iota(out[0], pattern, base, cm), [], [out])

    others = [T.cores[(rank + k) % N] for k in range(1, N)]
    far = [c for c in others if topo.die(c) != topo.die(core)]
    near = [c for c in others if topo.die(c) == topo.die(core)]
    eng = topo.engines(core, others[0])
    half = len(eng) // 2
    mask_far = sum(1 << e for e in eng[0::2])
    mask_near = sum(1 << e for e in eng[1::2])
    sent = [0]

    def send(e, src):
        def fn():
            trs = []
            for dsts, mask in ((far, mask_far), (near, mask_near)):
                ids = [DstId(rid=topo.addr(c)[0], pnc=topo.addr(c)[1]) for c in dsts]
                trs.append(RemoteDMATransfer(dst_ids=ids, dma_engine_mask=mask, remote_sem=T.sem["arr%d" % e],
                                             srcs=[src[0]], dsts=[src[0]] * len(dsts)))
            g.remote_dma_fused(trs, local_sem=T.sem.sent)
        add("G", fn, [src], [])
        sent[0] += 2 * half

    def arrive(e, pieces, win, base, n):
        w = [v(win, base + a, base + b) for a, b in ((0, rank * n), (rank * n + n, N * n)) if b > a]
        add(None, None, [], w, sem="arr%d" % e, total=(N - 1) * half * pieces)

    def own(e, a=0, b=V, st=1):
        return v("W%d" % e, o0 + a, o0 + b, st)

    def f(name):
        return v(name, 0, SCRATCH[name][1][1])

    add("S", lambda: g.sync.dma_start(T.AI[:], T.amp[:]), [], [f("AI")], sem="ldA")
    add("S", lambda: g.sync.dma_start(T.TI[:], T.tri[:]), [], [f("TI")], sem="ldT")
    add("S", lambda: g.sync.dma_start(T.PI[:], T.phi[:]), [], [f("PI")], sem="ldP")
    iota(f("J4"), [[16, 8], [1000, 2], [2, 8]], 0, -1)
    iota(f("J1"), [[1, 128]], 0, -1)
    iota(v("IP", 0, 1), [[0, 1]], 0, 1, False)
    iota(f("J2"), [[0, 8], [1, 16]], 0, 0)
    iota(f("J3"), [[1, 8], [0, 16]], 0, 0)
    ms(f("CSU"), -31.0 / 64)
    for n_, c_ in (("pA0", 0.0), ("pA1", 1000.0), ("pB0", -1.0), ("pB1", 999.0)):
        ts(f(n_), f("J4"), c_, ALU.is_equal)
    ts(f("fI"), f("J1"), 0.0, ALU.is_equal)
    ts(v("IQ", 0, 1), v("IP", 0, 1), 15, ALU.bitwise_and)
    ts(v("IQ", 1, 2), v("IP", 0, 1), 4, ALU.arith_shift_right)
    ms(f("CM"), M)
    cp(v("COL", 0, 2), v("IQ", 0, 2))
    ms(f("CK"), H)
    ts(f("fS"), f("J2"), v("COL", 0, 1), ALU.is_equal)
    ts(f("fG"), f("J3"), v("COL", 1, 2), ALU.is_equal, KS, ALU.mult)
    cp(own(0), f("AI"))
    send(0, own(0))
    arrive(0, 1, "W0", 0, V)
    iota(f("B3"), [[3, 128]], 0, 0)
    add("G", lambda: g.dma_start(T.THI[:, 0:1], T.th[:], allow_slow_non_contiguous=True), [], [v("THI", 0, 1)], sem="ldH")

    def permute(src, n, bank="P7"):
        h = n // 2
        for k, x in enumerate("AB"):
            mm(v(bank, k * h, k * h + h), "p%s0" % x, v(src, 0, n, 2), True, False)
            mm(v(bank, k * h, k * h + h), "p%s1" % x, v(src, 1, n, 2), False, True)

    prt = list(zip(R0_P, R0_P[1:]))

    def sums(k):
        n = prt[k][1] - prt[k][0]
        return ((("P0", 0), ("P0", n), ("P2", 0)), (("P1", 0), ("P1", n), ("P3", 0)),
                (("P5", 0), ("P7", 0), ("P6", 0)))[k]

    def r0_init(ps, parts=(0, 1, 2)):
        for k in parts:
            n = prt[k][1] - prt[k][0]
            s_, u_, k_ = sums(k)
            mm(v(s_[0], 0, 2 * n), "mI", v("CSU", 0, 2 * n), True, False)
            if u_[0] != s_[0]:
                mm(v(u_[0], 0, n), "mI", v("CSU", 0, n), True, False)
            mm(v(k_[0], 0, n), "mI", v("PRE", 256, 256 + n), True, False)
        for k, (a, b) in enumerate(prt if ps else []):
            mm(v(sums(k)[2][0], 0, b - a), "mI", v("COX", a, b), False, False)

    cp(f("TF"), f("TI"))
    permute("TF", V)
    for k, x in enumerate("AB"):
        for d, (lo, hi) in enumerate(KEPT):
            mm(v("P%d" % (5 + k), d, V, 3), "p%s0" % x, v("TF", lo, V, 3), True, False)
            mm(v("P%d" % (5 + k), d, V, 3), "p%s1" % x, v("TF", hi, V, 3), False, True)
    cp(f("PF"), f("PI"))
    act(f("mI"), f("fI"))
    act(f("mI8"), f("fI"), ACT.Identity, scale=0.125)
    act(f("J1"), f("fI"), ACT.Identity, scale=8.0)
    act(f("mS32"), f("fS"), ACT.Identity, scale=1.0 / 32)
    act(f("mGp"), f("fG"))
    act(f("mGn"), f("fG"), ACT.Identity, scale=-1.0)
    act(f("J2"), f("fS"), ACT.Identity, bias=-1.0)
    for q in range(3):
        ms(v("PRE", 256 + q, 512, 3), q * H)
        ms(v("OFC", q, V, 3), (q - 3) * CO)
    ts(v("P4", 0, V), f("PF"), 128.0, ALU.is_gt, -256.0, ALU.mult)
    ms(f("RST"), -BIG)
    tt(f("CS"), v("P4", 0, V), f("PF"), ALU.add)
    cp(f("L0"), v("P7", 0, V))
    ms(v("RST", 0, V, 3), BIG)
    ms(f("CX"), -KS / 2)
    ms(f("COX"), 0.0)
    r0_init(0, (0, 1))
    act(f("TA"), v("P5", 0, V))
    for s_ in range(16):
        ts(v("DG", NB * s_, NB * s_ + NB), f("mI"), v("fS", s_, s_ + 1), ALU.mult, -8192.0, ALU.mult)
    tt(f("BD0"), f("B3"), f("fS"), ALU.mult)
    tt(f("mMx"), f("J1"), f("fS"), ALU.add)
    tt(f("BE1"), f("BD0"), f("fS"), ALU.add)
    tt(f("BD1"), f("BE1"), f("J2"), ALU.add)
    tt(f("BD2"), f("BD1"), f("fS"), ALU.add)

    WA, WB = v("WX", 0, 8), v("WX", 8, 16)

    def round0(e):
        w = v("W%d" % e, 0, W)

        def direct(a, b):
            k = [j for j, (x, y) in enumerate(prt) if x <= a < y][0]
            s_, u_, k_ = sums(k)
            o = a - prt[k][0]
            for x, mat in ((k_, "mGp"), (s_, "mI8"), (u_, "mS32")):
                for m in range(8):
                    mm(v(x[0], x[1] + o, x[1] + o + b - a), mat, v("MN", 8 * a + m, 8 * b, 8), False,
                       m == 7 and b == prt[k][1] and not (x is s_ and s_[0] == u_[0]))

        def at(x, k, q=0, st=1):
            return v(x[0], x[1] + q, x[1] + prt[k][1] - prt[k][0], st)

        def sc(k):
            scan(v("RUN", *prt[k]), v("RST", *prt[k]), at(sums(k)[2], k), 0.0, ALU.max, ALU.min)

        def gaps(k):
            a, b = prt[k]
            for q in range(3):
                tt(v("P4", a + q, b, 3), at(sums(k)[2], k, q, 3), v("RUN", a + 2, b, 3), ALU.subtract)

        def t1(k):
            tt(v("T1", *prt[k]), at(sums(k)[0], k), own(e, *prt[k]), ALU.min)

        def t2(k):
            tt(v("T2", *prt[k]), at(sums(k)[1], k), v("T1", *prt[k]), ALU.min)

        def out(k):
            tt(own(e + 1, *prt[k]), v("P4", *prt[k]), v("T2", *prt[k]), ALU.min)

        def xs(k):
            send(e + 1, own(e + 1, prt[1][0], V) if k else own(e + 1, *prt[0]))

        steps = {"c": sc, "y": gaps, "u": t1, "w": t2, "o": out, "x": xs}
        for a, b in zip(R0_A, R0_A[1:]):
            (act if a else cp)(v("GA", 8 * a, 8 * b), ind(w, v("L0", a // 2, b // 2)))
        if e == 0:
            act(f("TC"), v("P6", 0, V))
            act(own(4), own(0))
        for i, (a, b) in enumerate(zip(R0_V, R0_V[1:])):
            tt(v("MN", 8 * a, 8 * b), ind(w, v("L0", (V + a) // 2, (V + b) // 2)), v("GA", 8 * a, 8 * b), ALU.min)
            if b in R0_G:
                direct(R0_G[R0_G.index(b) - 1], b)
            if b == R0_P[2] and e == 0:
                r0_init(0, (2,))
            for step in R0_TAIL.get(i, "").split():
                steps[step[0]](int(step[1]))
        arrive(e + 1, 2, "W%d" % (e + 1), 0, V)

    def prep_round1(ps):
        x = v("P7", 0, NB)
        tt(x, v("P4", 0, V, 3), f("fS"), ALU.min)
        tt(f("DL"), f("BD2"), v("P4", 2, V, 3), ALU.subtract)
        tt(f("D1"), x, f("BD0"), ALU.add)
        tt(v("P7", NB, 2 * NB), v("P4", 2, V, 3), f("BD2"), ALU.min)
        scan(f("SC"), f("DL"), f("D1"), 0.0, ALU.max, ALU.max)
        act(f("SG1"), v("P4", 0, V, 3), ACT.Sign, bias=1.0, scale=-1.0)
        act(v("P4", 0, V), v("P4", 0, V), ACT.Identity, bias=3 * H, scale=-4.0)
        tt(f("LM"), f("BD1"), x, ALU.subtract)
        cp(WB, v("SC", 15, NB, 16))
        tt(f("HH"), v("P7", NB, 2 * NB), f("BE1"), ALU.max)
        cp(v("L1", 0, NB), ind(f("TA"), WB))
        cp(v("L1", NB, 256), ind(f("TC"), WB))
        if ps:
            act(f("OL"), ind(f("DCX"), WB))
            ts(f("WB1"), v("SC", 79, NB, 16), -(V // 2) * 1.0, ALU.add)
        act(f("TB"), ind(f("TF"), WB))
        tt(f("CSH"), v("P4", 0, V), f("CS"), ALU.max)
        for k, (b0, b1) in enumerate(R1_CHUNKS):
            d = v("P%d" % (5 + k), b0, b1)
            mm(d, "mI", v("CK", b0, b1), True, False)
            if ps:
                mm(d, "mI", v("OL", b0, b1), False, False)
        permute("TB", NB, "P4")

    def round1(e):
        w = v("W%d" % e, 0, W)

        def post(k):
            b0, b1 = R1_CHUNKS[k]
            p = "P%d" % (5 + k)
            E, F, Y = v(p, 128 + b0, 128 + b1), v(p, 256 + b0, 256 + b1), v(p, 384 + b0, 384 + b1)
            ts(E, v(p, b0, b1), H, ALU.min, -H, ALU.max)
            ts(F, v(p, b0, b1), -1.0, ALU.mult, H, ALU.min)
            tt(Y, E, v("SG1", b0, b1), ALU.mult)
            for q, x in ((0, E), (2, F), (1, Y)):
                tt(own(e + 1, 3 * b0 + q, 3 * b1, 3), x, v("CSH", 3 * b0 + q, 3 * b1, 3), ALU.max)
            send(e + 1, own(e + 1, 3 * b0, 3 * b1))

        for a, b in zip(R1_A, R1_A[1:]):
            (act if a else cp)(v("GA", 16 * a, 16 * b), ind(w, v("L1", a, b)))
        act(v("NCS", NB, 256), ind(f("CS"), WB), ACT.Identity, scale=-1.0)
        act(f("LF"), v("P4", 0, NB))
        if e == 1:
            act(v("AS", NB, 256), ind(own(0), WB))
        else:
            act(v("C64", NB, 256), v("NCS", NB, 256), ACT.Identity, scale=-64.0)
            act(v("CU", NB, 256), ind(f("PF"), WB))
        for i, (a, b) in enumerate(zip(R1_V, R1_V[1:])):
            tt(v("MN", 16 * a, 16 * b), ind(w, v("L1", NB + a, NB + b)), v("GA", 16 * a, 16 * b), ALU.min)
            if b in R1_G:
                a = R1_G[R1_G.index(b) - 1]
                k = int(a >= R1_CHUNKS[1][0])
                for m in range(16):
                    mm(v("P%d" % (5 + k), a, b), "mGp" if m >= 8 else "mGn", v("MN", 16 * a + m, 16 * b, 16), False,
                       m == 15 and b == R1_CHUNKS[k][1])
            if i == R1_POST:
                post(0)
        post(1)
        arrive(e + 1, len(R1_CHUNKS), "W%d" % (e + 1), 0, V)

    def fill(o, banks):
        for k in banks:
            if k < 4:
                mm(v("P%d" % k, 0, 256), "mI", f("CM"), True, False)
                for m in range(8):
                    mm(v("P%d" % k, m, 256, 8), "mI", v("NCS", o + 32 * k, o + 32 * k + 32), False, False)
            else:
                mm(v("P%d" % k, 0, NB), "mI", v("C64", o, o + NB) if k == 5 else f("CX"), True, False)

    def prep_levels(ps):
        cp(WA, v("SC", 15, NB, 16))
        cp(f("TS"), ind(f("TF"), WA))
        act(v("NCS", 0, NB), ind(f("CS"), WA), ACT.Identity, scale=-1.0)
        permute("TS", NB)
        cp(f("L3"), v("P4", 0, NB))
        ts(f("ALT"), v("P4", 0, NB), 1.0 / 3, ALU.mult, W - 1.0 / 3, ALU.add)
        if ps == 0:
            cp(v("COL", 2, 3), v("THI", 0, 1))
        cp(f("ALF"), f("ALT"))
        if ps == 0:
            ts(f("mGt"), f("fG"), v("COL", 2, 3), ALU.mult, -1.0, ALU.mult)
        cp(f("L2"), v("P7", 0, NB))
        act(v("C64", 0, NB), v("NCS", 0, NB), ACT.Identity, scale=-64.0)
        fill(0, (0, 1, 2, 3, 5, 6))
        if ps == 0:
            act(v("AS", 0, NB), ind(own(0), WA))
        else:
            act(v("CU", 0, NB), ind(f("PF"), WA))
            act(f("LEV"), own(6), ACT.Relu, bias=2.0, scale=-1.0 / H)
            act(v("P4", 0, NB), v("CU", NB, 256))
            add("S", lambda: g.sync.dma_start(T.ylev[:], T.LEV[0:128:16, :]), [f("LEV")], [], sem="stL")

    def look(e, scalar):
        for a, b in PF_A if scalar else PF_V:
            x, y = v("GA", 1024 + 16 * a, 1024 + 16 * b), ind(v("W%d" % e, 0, W), v("L3", a, b))
            if scalar:
                act(x, y, ACT.Abs, bias=-1.0, scale=1.0 / H)
            else:
                ts(x, y, H, ALU.not_equal)

    def turn(h):
        return v(("P7", "P4")[h], NB, NB + 64)

    def pick(h):
        mm(turn(h), "fI", v("ALF", 64 * h, 64 * h + 64), True, False)
        for s_ in range(16):
            mm(turn(h), v("DG", NB * s_, NB * s_ + NB), v("GA", 1024 * (h + 1) + s_, 1024 * (h + 2), 16), False, s_ == 15)

    def relist(h):
        tt(turn(h), turn(h), v("LF", 64 * h, 64 * h + 64), ALU.max)
        cp(v("L4", 64 * h, 64 * h + 64), turn(h))

    def level(w, lst, need_z, aside):
        pieces = list(zip(LV, LV[1:]))

        def q(name, k):
            return v(name, 256 * k, 256 * k + 256)

        def e_(k):
            return v("P%d" % k, 0, 256)

        def ga(k):
            a, b = pieces[k]
            (act if k else cp)(v("GA", 16 * a, 16 * b), ind(w, v(lst, a, b)))

        def s(k):
            a, b = pieces[k]
            tt(v("MN", 16 * a, 16 * b), ind(w, v(lst, 64 + a, 64 + b)), v("GA", 16 * a, 16 * b), ALU.add)
            if b % 16 == 0:
                mm(e_(b // 16 - 1), "mI", q("MN", b // 16 - 1), False, True)

        def r(k):
            act(q("NR", k), e_(k), ACT.Identity, bias=-0.5, scale=-1.0)

        def d(k):
            tt(q("DD", k), e_(k), q("NR", k), ALU.add)

        def ab(k):
            act(q("F2", k), q("DD", k), ACT.Abs)

        def vv(h):
            ts(v("VV", 512 * h, 512 * h + 512), v("MN", 512 * h, 512 * h + 512), 1000.0, ALU.is_lt)
            summ("P6", "mGt", "VV", h)

        def summ(bank, mat, src, h, stop=False):
            for m in range(8):
                mm(v(bank, 64 * h, 64 * h + 64), mat, v(src, 512 * h + m, 512 * h + 512, 8), False, stop and m == 7)

        def zz(h):
            if need_z:
                summ("P5", "mMx", "DD", h, h == 1)

        def xx(h):
            summ("P6", "mGp", "F2", h, h == 1)

        def by(k):
            if k in aside:
                aside[k]()

        calls_ = {"g": ga, "s": s, "r": r, "d": d, "a": ab, "v": vv, "z": zz, "x": xx, "b": by}
        for step in ORDER.split():
            calls_[step[0]](int(step[1]))

    Z, X = v("P5", 0, NB), v("P6", 0, NB)

    def new_phase(zi, yi, shift):
        ts(f(zi), Z, 64.0 * shift, ALU.add)
        ts(f(yi), f(zi), 6, ALU.arith_shift_right, 255, ALU.bitwise_and)

    for ps in range(2):
        e = 4 * ps
        round0(e)
        prep_round1(ps)
        round1(e + 1)
        for k, (b0, b1) in enumerate(R1_CHUNKS):
            tt(v("D1", b0, b1), v("P%d" % (5 + k), 256 + b0, 256 + b1), v("HH", b0, b1), ALU.min)
        scan(f("SC"), f("LM"), f("D1"), 0.0, ALU.max, ALU.max)
        prep_levels(ps)
        win = "W%d" % (e + 2)
        level(v(win, 0, W), "L2", True, {})
        look(e + 2, True)
        new_phase("ZI", "YI", 127)
        if ps:
            cp(f("ZJ"), Z)
        ts(v("P6", NB, 2 * NB), X, H, ALU.min, -127.0, ALU.max)
        val = v(win, W + rank * NB, W + rank * NB + NB)
        tt(val, v("P6", NB, 2 * NB), f("YI"), ALU.add)
        send(e + 3, val)
        arrive(e + 3, 1, win, W, NB)
        fill(NB, (0, 1))
        look(e + 2, False)
        pick(0)
        pick(1)
        fill(NB, (2, 3, 5, 6) if ps else (2, 3, 6))
        ts(f("AC1"), val, 1000.0, ALU.is_lt)
        relist(0)
        if ps:
            ts(f("YJ"), f("ZJ"), 6, ALU.arith_shift_right, 255, ALU.bitwise_and)
        relist(1)
        if ps == 0:
            level(f(win), "L4", False, {2: lambda: tt(ind(own(4), WA), v("AS", 0, NB), f("AC1"), ALU.mult)})
            ts(f("AC0"), X, 0.0, ALU.is_le)
            tt(ind(own(4), WB), v("AS", NB, 256), f("AC0"), ALU.mult)
            send(4, own(4))
            arrive(4, 1, "W4", 0, V)
            act(f("OC"), ind(f("OFC"), f("WX")))
            ts(f("RJ0"), X, 0.0, ALU.is_gt)
            ts(f("RJ1"), val, 1000.0, ALU.is_gt)
            tt(ind(f("COX"), WA), v("OC", 0, NB), f("RJ1"), ALU.mult)
            tt(ind(f("COX"), WB), v("OC", NB, 256), f("RJ0"), ALU.mult)
            for d, (lo, hi) in enumerate(KEPT):
                tt(v("DCX", d, V, 3), v("COX", hi, V, 3), v("COX", lo, V, 3), ALU.subtract)
            r0_init(1)
        else:
            level(f(win), "L4", True, {0: lambda: tt(f("DT"), f("YJ"), v("CU", 0, NB), ALU.subtract),
                                       1: lambda: tt(f("DE"), f("DT"), f("AC1"), ALU.mult),
                                       2: lambda: tt(ind(f("PF"), WA), f("DE"), v("CU", 0, NB), ALU.add)})
            new_phase("ZI", "YI", 0)
            tt(f("DT"), f("YI"), v("P4", 0, NB), ALU.subtract)
            ts(v("P6", NB, 2 * NB), X, 0.0, ALU.is_le)
            tt(f("DE"), v("P6", NB, 2 * NB), f("DT"), ALU.mult)
            hv = V // 2
            tt(ind(v("PF", 0, hv), v("WX", 8, 12)), v("DE", 0, 64), v("CU", NB, NB + 64), ALU.add)
            add("S", lambda: g.sync.dma_start(T.yphi[:, 0:hv], T.PF[:, 0:hv]), [v("PF", 0, hv)], [], sem="stP0")
            tt(ind(v("PF", hv, V), f("WB1")), v("DE", 64, NB), v("CU", NB + 64, 256), ALU.add)
            add("A", lambda: g.scalar.dma_start(T.yphi[:, hv:V], T.PF[:, hv:V]), [v("PF", hv, V)], [], sem="stP1")

    n = {q: 0 for q in queues}
    for op in ops:
        if op["sem"] is None:
            if op["mark"]:
                n[op["q"]] += 1
            op["wait"] = ("c" + op["q"], n[op["q"]])
        else:
            op["wait"] = (op["sem"], op["total"])
    for op in ops:
        if op["q"] is None:
            continue
        for o2 in op["waits"]:
            queues[op["q"]].wait_ge(T.sem[o2["wait"][0]], o2["wait"][1])
        ins = op["fn"]()
        if op["sem"] is not None:
            ins.then_inc(T.sem[op["sem"]], 16)
        elif op["mark"]:
            ins.then_inc(T.sem["c" + op["q"]], 1)
    g.wait_ge(T.sem.sent, sent[0])
    g.sync.wait_ge(T.sem.stL, 16)
    g.sync.wait_ge(T.sem.stP0, 16)
    g.sync.wait_ge(T.sem.stP1, 16)
